import numpy as np
import ml_dtypes


def mxq(x, axis, fmt="e4m3"):
    dtype, down = {"e4m3": (ml_dtypes.float8_e4m3fn, 7), "e5m2": (ml_dtypes.float8_e5m2, 14)}[fmt]
    v = np.moveaxis(np.asarray(x, np.float32).astype(ml_dtypes.bfloat16).astype(np.float64), axis, -1)
    blocks = v.reshape(v.shape[:-1] + (-1, 32))
    amax = np.abs(blocks).max(-1, keepdims=True)
    byte = np.maximum(np.where(amax > 0, np.frexp(amax)[1] - 1 + 127, 0) - down, 1)
    scale = np.exp2(byte - 127.0)
    codes = (blocks / scale).astype(np.float32).astype(dtype).astype(np.float64)
    return np.moveaxis((codes * scale).reshape(v.shape), -1, axis)


WIDE = False


def mx_kscale(k):
    if not WIDE:
        return np.ones(k)
    levels = np.array([24, -24, 12, -12, 0])
    if k % 512:
        return np.exp2(np.random.permutation(np.resize(levels, k // 32))).repeat(32)
    a = np.empty((k // 512, 16))
    for p in range(k // 512):
        a[p, :8] = np.random.permutation(np.resize(levels, 8))
        for g in range(8):
            far = levels[np.abs(levels - a[p, g]) >= 10]
            a[p, g + 8] = far[np.random.randint(len(far))]
    return np.exp2(a.ravel()).repeat(32)


def f64(x):
    return np.asarray(x).astype(np.float64)


def striped(idx):
    return np.tile(idx.reshape(-1, 16).T, (8, 1)).astype(np.uint16)


def unstriped(offs):
    return offs[:16].T.reshape(-1).astype(np.int64)


E2M1 = np.array([0.0, 0.5, 1.0, 1.5, 2.0, 3.0, 4.0, 6.0, -0.0, -0.5, -1.0, -1.5, -2.0, -3.0, -4.0, -6.0])


def pack_weight(w, fmt):
    k, n = w.shape
    w = f64(np.asarray(w, np.float32).astype(ml_dtypes.bfloat16)).reshape(k // 32, 32, n)
    amax = np.abs(w).max(1)
    if fmt == "e4m3":
        byte = np.frexp(amax)[1] - 1 + 127 - 7
    else:
        mant, ex = np.frexp(amax / 6.0)
        byte = np.where(mant > 0.5, ex, ex - 1) + 127
    byte = np.clip(np.where(amax > 0, byte, 1), 1, 254)
    scaled = (w * np.exp2(127.0 - byte)[:, None, :]).reshape(k, n).astype(np.float32)
    by_word = np.ascontiguousarray(scaled.reshape(k // 512, 128, 4, n).transpose(0, 1, 3, 2))
    if fmt == "e4m3":
        words = by_word.astype(ml_dtypes.float8_e4m3fn).view(np.uint8)
    else:
        c = by_word.astype(ml_dtypes.float4_e2m1fn).view(np.uint8) & 0xF
        words = (c[..., 0::2] | (c[..., 1::2] << 4)).reshape(k // 512, 128, 2 * n)
    return np.ascontiguousarray(words), np.ascontiguousarray(byte.astype(np.uint8).reshape(k // 512, 16, n))


def unpack_weight(words, scales, fmt):
    g, _, n = scales.shape
    words = np.ascontiguousarray(words).reshape(g, 128, n, -1)
    if fmt == "e4m3":
        vals = words.view(ml_dtypes.float8_e4m3fn).astype(np.float64)
    else:
        nib = np.empty((g, 128, n, 4), np.uint8)
        nib[..., 0::2] = words & 0xF
        nib[..., 1::2] = words >> 4
        vals = E2M1[nib]
    vals = vals * np.repeat(np.exp2(scales.astype(np.float64) - 127.0), 8, axis=1)[..., None]
    return vals.transpose(0, 1, 3, 2).reshape(g * 512, n)


def pack_table4(v):
    words, scales = pack_weight(v, "e2m1")
    g, t = words.shape[0] // 2, v.shape[1]
    return np.ascontiguousarray(words.reshape(g, 2, 128, t, 2).transpose(0, 2, 3, 1, 4).reshape(g, 128, t, 4)), scales


def unpack_table4(words, scales):
    g, _, t, _ = words.shape
    return unpack_weight(words.reshape(g, 128, t, 2, 2).transpose(0, 3, 1, 2, 4).reshape(2 * g, 128, 2 * t), scales, "e2m1")


K, R, N, T, J = 1024, 512, 512, 4096, 512


def setup_inputs():
    n = np.random.standard_normal
    s = mx_kscale(K)[:, None]
    u = mx_kscale(R)[:, None]
    p_tab = pack_table4(n((K, T)) * s)
    p_wc = pack_weight(n((K, R)) / np.sqrt(K) / s * u.T, "e2m1")
    return {
        "tab_words": p_tab[0],
        "tab_scales": p_tab[1],
        "c": (n((K, J)) * s).astype(np.float32),
        "w": (n((K, R)) / np.sqrt(K) / s * u.T).astype(np.float32),
        "wc_words": p_wc[0],
        "wc_scales": p_wc[1],
        "wd": (n((R, N)) / np.sqrt(R) / u).astype(np.float32),
        "gm": (n((N, J))).astype(np.float32),
        "offs": striped(np.concatenate([np.random.permutation(T)[:J] for _ in range(4)])),
    }


def reference(tab_words, tab_scales, c, w, wc_words, wc_scales, wd, gm, offs):
    idx = unstriped(offs).reshape(4, J)
    tab_ = unpack_table4(tab_words, tab_scales)[:, idx]
    c_ = mxq(f64(c), 0, "e4m3")
    w_ = mxq(f64(w), 0, "e4m3")
    a0 = w_.T @ tab_[:, 0]
    a1 = w_.T @ tab_[:, 1]
    a2 = w_.T @ tab_[:, 2]
    a3 = w_.T @ tab_[:, 3]
    wc_ = unpack_weight(wc_words, wc_scales, "e2m1")
    ac = wc_.T @ c_
    h = np.maximum(np.maximum(np.maximum(np.maximum(a0, a1), a2), a3) + ac, 0.0)
    h_ = mxq(h, 0, "e4m3")
    wd_ = mxq(f64(wd), 0, "e4m3")
    y = wd_.T @ h_
    return y * f64(gm)

@@ -1,0 +1,260 @@
+from contextlib import ExitStack
+
+import concourse.mybir as mybir
+
+K, R, N, T, J = 1024, 512, 512, 4096, 512
+G = 4
+FLOPS = 2 * (G + 1) * K * R * J + 2 * R * N * J
+
+F32 = mybir.dt.float32
+BF16 = mybir.dt.bfloat16
+I32 = mybir.dt.int32
+U32 = mybir.dt.uint32
+U16 = mybir.dt.uint16
+U8 = mybir.dt.uint8
+FP8X4 = mybir.dt.float8_e4m3fn_x4
+FP4X4 = mybir.dt.float4_e2m1fn_x4
+ACT = mybir.ActivationFunctionType
+ALU = mybir.AluOpType
+
+P = 128
+PACK = 4
+K_PASS = P * PACK
+PASSES = K // K_PASS
+HALF = 256
+CHUNK = 128
+CHUNKS = J // CHUNK
+LIST_COLS = J // 16
+
+
+def tile_list_pnet_gate_kernel(
+    tc, tab_words, tab_scales, c, w, wc_words, wc_scales, wd, gm, offs, out
+):
+    nc = tc.nc
+    with ExitStack() as ctx:
+        keep = ctx.enter_context(tc.tile_pool(name="keep", bufs=1))
+        stage = ctx.enter_context(tc.tile_pool(name="stage", bufs=4))
+        psum = ctx.enter_context(tc.psum_pool(name="psum", bufs=8))
+
+        offsets = keep.tile([P, G * LIST_COLS], U16, name="offsets")
+        nc.sync.dma_start(offsets[:], offs)
+
+        scale_rows = keep.tile([P, T // 4], I32, name="scale_rows", align_bytes=64)
+        nc.sync.dma_start(scale_rows[0:32, :], tab_scales.rearrange("a q t -> q a t").bitcast(I32))
+        nc.vector.memset(scale_rows[32:64, :], 0)
+        nc.vector.memset(scale_rows[64:128, :], 0)
+
+        table = keep.tile([P, T], I32, name="table", tag="table", align_bytes=64)
+        nc.sync.dma_start(table[:], tab_words[0].rearrange("p t b -> p (t b)").bitcast(I32))
+
+        def load_half(src, a, half):
+            raw = stage.tile([P, PACK, HALF], F32, name="raw", tag="stage", align_bytes=64)
+            rows = src[a * K_PASS : (a + 1) * K_PASS, half * HALF : (half + 1) * HALF]
+            nc.sync.dma_start(raw[:], rows.rearrange("(p j) x -> p j x", j=PACK))
+            return raw
+
+        w_codes = keep.tile([P, PASSES, R], U32, name="w_codes", align_bytes=64)
+        w_scales = keep.tile([P, PASSES, R], U8, name="w_scales", align_bytes=64)
+        w_bfs = []
+        for a in range(PASSES):
+            w_bf = keep.tile([P, R * PACK], BF16, name=f"w_bf{a}", align_bytes=64)
+            dst = w_bf[:].rearrange("p (t h i j) -> p h t j i", t=4, i=4, j=PACK)
+            for half in range(2):
+                raw = load_half(w, a, half)
+                src = raw[:].rearrange("p j (h t i) -> p h t j i", t=4, i=4)
+                part = dst[:, 16 * half : 16 * half + 16]
+                if a == 0 and half == 0:
+                    for t in range(4):
+                        nc.scalar.activation(part[:, :, t], src[:, :, t], ACT.Copy)
+                else:
+                    nc.scalar.copy(part, src)
+            w_bfs.append(w_bf)
+
+        def quantize_w(a):
+            nc.vector.quantize_mx(w_codes[:, a, :].bitcast(FP8X4), w_scales[:, a, :], w_bfs[a][:])
+
+        picked_scales = keep.tile([P, G * J], U8, name="picked_scales", align_bytes=64)
+        for s in range(2):
+            nc.vector.tensor_copy(
+                picked_scales[:, s * 2 * J : (s + 1) * 2 * J],
+                scale_rows[:].bitcast(U8).indirect(offsets[:, s * 2 * LIST_COLS : (s + 1) * 2 * LIST_COLS]),
+            )
+        planes = keep.tile([P, PASSES, G * J // 4], I32, name="planes", align_bytes=64)
+        nc.vector.memset(planes[:], 0)
+        for q in range(4):
+            nc.sync.dma_start(planes[32 * q : 32 * q + 4], picked_scales[8 * q : 8 * q + 8, :].bitcast(I32))
+        tab_planes = planes[:].bitcast(U8)
+
+        parted = []
+        for g in range(G):
+            picked = keep.tile([P, J], U32, name=f"picked{g}", align_bytes=64)
+            nc.vector.tensor_copy(
+                picked[:], table[:].bitcast(U32).indirect(offsets[:, g * LIST_COLS : (g + 1) * LIST_COLS])
+            )
+            if g == 3:
+                quantize_w(1)
+            words = keep.tile([P, PASSES, 2 * J], U8, name=f"words{g}", align_bytes=64)
+            nc.vector.tensor_copy(
+                words[:].bitcast(U16), picked[:].bitcast(U16).rearrange("p (n d) -> p d n", d=PASSES)
+            )
+            parted.append(words)
+            if g == 1:
+                quantize_w(0)
+
+        def project(bank, g, t, a):
+            nc.tensor.matmul_mx(
+                out=bank[:],
+                lhsT=w_codes[:, a, t * P : (t + 1) * P].bitcast(FP8X4),
+                lhsT_scale=w_scales[:, a, t * P : (t + 1) * P],
+                rhs=parted[g][:, a, :].bitcast(FP4X4),
+                rhs_scale=tab_planes[:, a, g * J : (g + 1) * J],
+                start=(a == 0),
+                stop=(a == PASSES - 1),
+            )
+
+        def new_banks(g):
+            return [psum.tile([P, J], F32, name=f"a{g}_{t}", tag="bank") for t in range(4)]
+
+        banks = [new_banks(0), new_banks(1)]
+        for g in range(2):
+            for t in range(4):
+                project(banks[g][t], g, t, 0)
+        for t in range(4):
+            for g in range(2):
+                project(banks[g][t], g, t, 1)
+        best = keep.tile([P, 4, J], F32, name="best0")
+        for t in range(4):
+            nc.scalar.copy(best[:, t, :], banks[0][t][:])
+
+        c_codes = keep.tile([P, 2, PASSES, HALF], U32, name="c_codes", align_bytes=64)
+        c_scales = keep.tile([P, 2, PASSES, HALF], U8, name="c_scales", align_bytes=64)
+        c_bfs = []
+        for half in range(2):
+            c_bf = keep.tile([P, PASSES, HALF * PACK], BF16, name=f"c_bf{half}", align_bytes=64)
+            for a in range(PASSES):
+                raw = load_half(c, a, half)
+                nc.scalar.copy(
+                    c_bf[:, a, :].rearrange("p (x i j) -> p x j i", i=4, j=PACK),
+                    raw[:].rearrange("p j (x i) -> p x j i", i=4),
+                )
+            c_bfs.append(c_bf)
+
+        def quantize_c(half):
+            nc.vector.quantize_mx(
+                c_codes[:, half].rearrange("p a x -> p (a x)").bitcast(FP8X4),
+                c_scales[:, half].rearrange("p a x -> p (a x)"),
+                c_bfs[half][:].rearrange("p a x -> p (a x)"),
+            )
+
+        wc_raw = stage.tile([P, PASSES, R // 2], I32, name="wc_raw", tag="stage", align_bytes=64)
+        nc.sync.dma_start(wc_raw[:], wc_words.rearrange("a p b -> p a b").bitcast(I32))
+        wc_codes = keep.tile([P, PASSES, R // 2], I32, name="wc_codes", align_bytes=64)
+
+        wd_raw = keep.tile([P, PACK, N], F32, name="wd_raw", tag="table", align_bytes=64)
+        wd_rows = wd.rearrange("(h t i) n -> t h i n", t=4, i=4)
+        for t in range(4):
+            nc.sync.dma_start(wd_raw[:, t, :], wd_rows[t])
+
+        wcs_raw = stage.tile([P, PASSES, R // 4], I32, name="wcs_raw", tag="stage", align_bytes=64)
+        nc.vector.memset(wcs_raw[:], 0)
+        for q in range(4):
+            nc.sync.dma_start(
+                wcs_raw[32 * q : 32 * q + 4],
+                wc_scales[:, 4 * q : 4 * q + 4, :].rearrange("a r n -> r a n").bitcast(I32),
+            )
+        wc_planes = keep.tile([P, PASSES, R // 4], I32, name="wc_planes", align_bytes=64)
+
+        def order_wc():
+            nc.vector.tensor_copy(
+                wc_codes[:].rearrange("p a (t h x) -> p a t h x", t=4, x=2),
+                wc_raw[:].rearrange("p a (h t x) -> p a t h x", t=4, x=2),
+            )
+            nc.vector.tensor_copy(
+                wc_planes[:].rearrange("p a (t h) -> p a t h", t=4),
+                wcs_raw[:].rearrange("p a (h t) -> p a t h", t=4),
+            )
+
+        wd_bf = keep.tile([P, N * PACK], BF16, name="wd_bf", align_bytes=64)
+        nc.scalar.copy(
+            wd_bf[:].rearrange("p (x i t) -> p x t i", i=4, t=PACK),
+            wd_raw[:].rearrange("p t (x i) -> p x t i", i=4),
+        )
+        wd_codes = keep.tile([P, N], U32, name="wd_codes", align_bytes=64)
+        wd_scales = keep.tile([P, N], U8, name="wd_scales", align_bytes=64)
+
+        gate = stage.tile([P, 4, J], F32, name="gate", tag="stage", align_bytes=64)
+        nc.sync.dma_start(gate[:], gm.rearrange("(u p) j -> p u j", p=P))
+
+        for g in range(1, G):
+            if g >= 2:
+                banks.append(new_banks(g))
+                for t in range(4):
+                    for a in range(PASSES):
+                        project(banks[g][t], g, t, a)
+            merged = keep.tile([P, 4, J], F32, name=f"best{g}")
+            for t in range(4):
+                if (g, t) == (3, 2):
+                    quantize_c(1)
+                nc.vector.tensor_tensor(merged[:, t, :], banks[g][t][:], best[:, t, :], ALU.max)
+            best = merged
+            if g == 2:
+                quantize_c(0)
+                order_wc()
+
+        wc_bytes = wc_codes[:].bitcast(U8)
+        wc_scale_bytes = wc_planes[:].bitcast(U8)
+        h_bf = []
+        for ch in range(CHUNKS):
+            half, x0 = divmod(ch * CHUNK, HALF)
+            own = psum.tile([P, 4, CHUNK], F32, name=f"own{ch}", tag="bank")
+            for t in range(4):
+                for a in range(PASSES):
+                    nc.tensor.matmul_mx(
+                        out=own[:, t, :],
+                        lhsT=wc_bytes[:, a, 2 * t * P : 2 * (t + 1) * P].bitcast(FP4X4),
+                        lhsT_scale=wc_scale_bytes[:, a, t * P : (t + 1) * P],
+                        rhs=c_codes[:, half, a, x0 : x0 + CHUNK].bitcast(FP8X4),
+                        rhs_scale=c_scales[:, half, a, x0 : x0 + CHUNK],
+                        start=(a == 0),
+                        stop=(a == PASSES - 1),
+                    )
+            summed = keep.tile([P, 4, CHUNK], F32, name=f"summed{ch}")
+            nc.vector.tensor_tensor(summed[:], own[:], best[:, :, ch * CHUNK : (ch + 1) * CHUNK], ALU.add)
+            if ch == 1:
+                nc.vector.quantize_mx(wd_codes[:].bitcast(FP8X4), wd_scales[:], wd_bf[:])
+            hb = keep.tile([P, CHUNK * PACK], BF16, name=f"h_bf{ch}", align_bytes=64)
+            nc.scalar.activation(
+                hb[:].rearrange("p (x i t) -> p x t i", i=4, t=PACK),
+                summed[:].rearrange("p t (x i) -> p x t i", i=4),
+                ACT.Relu,
+            )
+            h_bf.append(hb)
+
+        out_rows = out.rearrange("(u p) j -> p u j", p=P)
+        ys = []
+
+        def finish(ch):
+            cols = slice(ch * CHUNK, (ch + 1) * CHUNK)
+            res = keep.tile([P, 4, CHUNK], F32, name=f"res{ch}")
+            nc.vector.tensor_tensor(res[:], ys[ch][:], gate[:, :, cols], ALU.mult)
+            nc.sync.dma_start(out_rows[:, :, cols], res[:])
+
+        for ch in range(CHUNKS):
+            h_codes = keep.tile([P, CHUNK], U32, name=f"h_codes{ch}", align_bytes=64)
+            h_scales = keep.tile([P, CHUNK], U8, name=f"h_scales{ch}", align_bytes=64)
+            nc.vector.quantize_mx(h_codes[:].bitcast(FP8X4), h_scales[:], h_bf[ch][:])
+            y = psum.tile([P, 4, CHUNK], F32, name=f"y{ch}", tag="bank")
+            for u in range(4):
+                nc.tensor.matmul_mx(
+                    out=y[:, u, :],
+                    lhsT=wd_codes[:, u * P : (u + 1) * P].bitcast(FP8X4),
+                    lhsT_scale=wd_scales[:, u * P : (u + 1) * P],
+                    rhs=h_codes[:].bitcast(FP8X4),
+                    rhs_scale=h_scales[:],
+                    start=True,
+                    stop=True,
+                )
+            ys.append(y)
+            if ch > 0:
+                finish(ch - 1)
+        finish(CHUNKS - 1)

@@ -33,13 +33,12 @@ def tile_list_pnet_gate_kernel(
     nc = tc.nc
     with ExitStack() as ctx:
         keep = ctx.enter_context(tc.tile_pool(name="keep", bufs=1))
-        stage = ctx.enter_context(tc.tile_pool(name="stage", bufs=4))
-        psum = ctx.enter_context(tc.psum_pool(name="psum", bufs=8))
+        psum = ctx.enter_context(tc.psum_pool(name="psum", bufs=1))
 
         offsets = keep.tile([P, G * LIST_COLS], U16, name="offsets")
         nc.sync.dma_start(offsets[:], offs)
 
-        scale_rows = keep.tile([P, T // 4], I32, name="scale_rows", align_bytes=64)
+        scale_rows = keep.tile([P, T // 4], I32, name="scale_rows", tag="rows", align_bytes=64)
         nc.sync.dma_start(scale_rows[0:32, :], tab_scales.rearrange("a q t -> q a t").bitcast(I32))
         nc.vector.memset(scale_rows[32:64, :], 0)
         nc.vector.memset(scale_rows[64:128, :], 0)
@@ -47,8 +46,8 @@ def tile_list_pnet_gate_kernel(
         table = keep.tile([P, T], I32, name="table", tag="table", align_bytes=64)
         nc.sync.dma_start(table[:], tab_words[0].rearrange("p t b -> p (t b)").bitcast(I32))
 
-        def load_half(src, a, half):
-            raw = stage.tile([P, PACK, HALF], F32, name="raw", tag="stage", align_bytes=64)
+        def load_half(src, a, half, tag):
+            raw = keep.tile([P, PACK, HALF], F32, name="raw", tag=tag, align_bytes=64)
             rows = src[a * K_PASS : (a + 1) * K_PASS, half * HALF : (half + 1) * HALF]
             nc.sync.dma_start(raw[:], rows.rearrange("(p j) x -> p j x", j=PACK))
             return raw
@@ -57,10 +56,10 @@ def tile_list_pnet_gate_kernel(
         w_scales = keep.tile([P, PASSES, R], U8, name="w_scales", align_bytes=64)
         w_bfs = []
         for a in range(PASSES):
-            w_bf = keep.tile([P, R * PACK], BF16, name=f"w_bf{a}", align_bytes=64)
+            w_bf = keep.tile([P, R * PACK], BF16, name=f"w_bf{a}", tag=f"w_bf{a}", align_bytes=64)
             dst = w_bf[:].rearrange("p (t h i j) -> p h t j i", t=4, i=4, j=PACK)
             for half in range(2):
-                raw = load_half(w, a, half)
+                raw = load_half(w, a, half, f"stage{2 * a + half}")
                 src = raw[:].rearrange("p j (h t i) -> p h t j i", t=4, i=4)
                 part = dst[:, 16 * half : 16 * half + 16]
                 if a == 0 and half == 0:
@@ -73,70 +72,81 @@ def tile_list_pnet_gate_kernel(
         def quantize_w(a):
             nc.vector.quantize_mx(w_codes[:, a, :].bitcast(FP8X4), w_scales[:, a, :], w_bfs[a][:])
 
-        picked_scales = keep.tile([P, G * J], U8, name="picked_scales", align_bytes=64)
+        picked_scales = keep.tile([P, G * J], U8, name="picked_scales", tag="picked_scales", align_bytes=64)
         for s in range(2):
             nc.vector.tensor_copy(
                 picked_scales[:, s * 2 * J : (s + 1) * 2 * J],
                 scale_rows[:].bitcast(U8).indirect(offsets[:, s * 2 * LIST_COLS : (s + 1) * 2 * LIST_COLS]),
             )
         planes = keep.tile([P, PASSES, G * J // 4], I32, name="planes", align_bytes=64)
-        nc.vector.memset(planes[:], 0)
+        nc.gpsimd.memset(planes[:], 0)
         for q in range(4):
             nc.sync.dma_start(planes[32 * q : 32 * q + 4], picked_scales[8 * q : 8 * q + 8, :].bitcast(I32))
         tab_planes = planes[:].bitcast(U8)
 
-        parted = []
-        for g in range(G):
-            picked = keep.tile([P, J], U32, name=f"picked{g}", align_bytes=64)
-            nc.vector.tensor_copy(
-                picked[:], table[:].bitcast(U32).indirect(offsets[:, g * LIST_COLS : (g + 1) * LIST_COLS])
-            )
-            if g == 3:
-                quantize_w(1)
-            words = keep.tile([P, PASSES, 2 * J], U8, name=f"words{g}", align_bytes=64)
-            nc.vector.tensor_copy(
-                words[:].bitcast(U16), picked[:].bitcast(U16).rearrange("p (n d) -> p d n", d=PASSES)
-            )
-            parted.append(words)
-            if g == 1:
-                quantize_w(0)
+        parted = {}
+        picked = {}
 
-        def project(bank, g, t, a):
+        def pick(g0, count, tag):
+            picked[g0] = keep.tile([P, count * J], U32, name=f"picked{g0}", tag=tag, align_bytes=64)
+            nc.vector.tensor_copy(
+                picked[g0][:],
+                table[:].bitcast(U32).indirect(offsets[:, g0 * LIST_COLS : (g0 + count) * LIST_COLS]),
+            )
+
+        def part_passes(g0, count, tag):
+            words = keep.tile([P, PASSES, 2 * count * J], U8, name=f"words{g0}", tag=tag, align_bytes=64)
+            nc.vector.tensor_copy(
+                words[:].bitcast(U16), picked[g0][:].bitcast(U16).rearrange("p (n d) -> p d n", d=PASSES)
+            )
+            for k in range(count):
+                parted[g0 + k] = words[:, :, 2 * k * J : 2 * (k + 1) * J]
+
+        pick(0, 2, "picked0")
+        pick(2, 1, "picked2")
+        part_passes(0, 2, "words0")
+        quantize_w(0)
+        part_passes(2, 1, "w_bf0")
+        quantize_w(1)
+        pick(3, 1, "w_bf1")
+        part_passes(3, 1, "words3")
+
+        def project(dst, g, t, a, j0=0, width=J):
             nc.tensor.matmul_mx(
-                out=bank[:],
+                out=dst,
                 lhsT=w_codes[:, a, t * P : (t + 1) * P].bitcast(FP8X4),
                 lhsT_scale=w_scales[:, a, t * P : (t + 1) * P],
-                rhs=parted[g][:, a, :].bitcast(FP4X4),
-                rhs_scale=tab_planes[:, a, g * J : (g + 1) * J],
+                rhs=parted[g][:, a, 2 * j0 : 2 * (j0 + width)].bitcast(FP4X4),
+                rhs_scale=tab_planes[:, a, g * J + j0 : g * J + j0 + width],
                 start=(a == 0),
                 stop=(a == PASSES - 1),
             )
 
         def new_banks(g):
-            return [psum.tile([P, J], F32, name=f"a{g}_{t}", tag="bank") for t in range(4)]
+            return [psum.tile([P, J], F32, name=f"a{g}_{t}", tag=f"bank{g % 2}{t}") for t in range(4)]
 
         banks = [new_banks(0), new_banks(1)]
-        for g in range(2):
-            for t in range(4):
-                project(banks[g][t], g, t, 0)
         for t in range(4):
-            for g in range(2):
-                project(banks[g][t], g, t, 1)
-        best = keep.tile([P, 4, J], F32, name="best0")
+            project(banks[0][t][:], 0, t, 0)
         for t in range(4):
-            nc.scalar.copy(best[:, t, :], banks[0][t][:])
+            project(banks[0][t][:], 0, t, 1)
+            project(banks[1][t][:], 1, t, 0)
+            project(banks[1][t][:], 1, t, 1)
 
         c_codes = keep.tile([P, 2, PASSES, HALF], U32, name="c_codes", align_bytes=64)
-        c_scales = keep.tile([P, 2, PASSES, HALF], U8, name="c_scales", align_bytes=64)
         c_bfs = []
         for half in range(2):
-            c_bf = keep.tile([P, PASSES, HALF * PACK], BF16, name=f"c_bf{half}", align_bytes=64)
+            c_bf = keep.tile([P, PASSES, HALF * PACK], BF16, name=f"c_bf{half}", tag=f"c_bf{half}", align_bytes=64)
             for a in range(PASSES):
-                raw = load_half(c, a, half)
+                raw = load_half(c, a, half, ("rows", "stage0", "stage1", "stage2")[2 * half + a])
                 nc.scalar.copy(
                     c_bf[:, a, :].rearrange("p (x i j) -> p x j i", i=4, j=PACK),
                     raw[:].rearrange("p j (x i) -> p x j i", i=4),
                 )
+                if (half, a) == (0, 0):
+                    best = keep.tile([P, 4, J], F32, name="best0", tag="rows", align_bytes=64)
+                    for t in range(4):
+                        nc.scalar.copy(best[:, t, :], banks[0][t][:])
             c_bfs.append(c_bf)
 
         def quantize_c(half):
@@ -146,7 +156,7 @@ def tile_list_pnet_gate_kernel(
                 c_bfs[half][:].rearrange("p a x -> p (a x)"),
             )
 
-        wc_raw = stage.tile([P, PASSES, R // 2], I32, name="wc_raw", tag="stage", align_bytes=64)
+        wc_raw = keep.tile([P, PASSES, R // 2], I32, name="wc_raw", tag="stage3", align_bytes=64)
         nc.sync.dma_start(wc_raw[:], wc_words.rearrange("a p b -> p a b").bitcast(I32))
         wc_codes = keep.tile([P, PASSES, R // 2], I32, name="wc_codes", align_bytes=64)
 
@@ -155,8 +165,8 @@ def tile_list_pnet_gate_kernel(
         for t in range(4):
             nc.sync.dma_start(wd_raw[:, t, :], wd_rows[t])
 
-        wcs_raw = stage.tile([P, PASSES, R // 4], I32, name="wcs_raw", tag="stage", align_bytes=64)
-        nc.vector.memset(wcs_raw[:], 0)
+        wcs_raw = keep.tile([P, PASSES, R // 4], I32, name="wcs_raw", tag="picked_scales", align_bytes=64)
+        nc.gpsimd.memset(wcs_raw[:], 0)
         for q in range(4):
             nc.sync.dma_start(
                 wcs_raw[32 * q : 32 * q + 4],
@@ -174,7 +184,8 @@ def tile_list_pnet_gate_kernel(
                 wcs_raw[:].rearrange("p a (h t) -> p a t h", t=4),
             )
 
-        wd_bf = keep.tile([P, N * PACK], BF16, name="wd_bf", align_bytes=64)
+        c_scales = keep.tile([P, 2, PASSES, HALF], U8, name="c_scales", align_bytes=64)
+        wd_bf = keep.tile([P, N * PACK], BF16, name="wd_bf", tag="wd_bf", align_bytes=64)
         nc.scalar.copy(
             wd_bf[:].rearrange("p (x i t) -> p x t i", i=4, t=PACK),
             wd_raw[:].rearrange("p t (x i) -> p x t i", i=4),
@@ -182,35 +193,46 @@ def tile_list_pnet_gate_kernel(
         wd_codes = keep.tile([P, N], U32, name="wd_codes", align_bytes=64)
         wd_scales = keep.tile([P, N], U8, name="wd_scales", align_bytes=64)
 
-        gate = stage.tile([P, 4, J], F32, name="gate", tag="stage", align_bytes=64)
+        gate = keep.tile([P, 4, J], F32, name="gate", tag="stage1", align_bytes=64)
         nc.sync.dma_start(gate[:], gm.rearrange("(u p) j -> p u j", p=P))
 
-        for g in range(1, G):
-            if g >= 2:
-                banks.append(new_banks(g))
-                for t in range(4):
-                    for a in range(PASSES):
-                        project(banks[g][t], g, t, a)
-            merged = keep.tile([P, 4, J], F32, name=f"best{g}")
+        def merge(g, best, tag):
+            merged = keep.tile([P, 4, J], F32, name=f"best{g}", tag=tag, align_bytes=64)
             for t in range(4):
-                if (g, t) == (3, 2):
-                    quantize_c(1)
+                if (g, t) == (2, 2):
+                    quantize_c(0)
                 nc.vector.tensor_tensor(merged[:, t, :], banks[g][t][:], best[:, t, :], ALU.max)
-            best = merged
-            if g == 2:
-                quantize_c(0)
-                order_wc()
+            return merged
+
+        best = merge(1, best, "best1")
+        order_wc()
+        banks.append(new_banks(2))
+        for t in range(4):
+            for a in range(PASSES):
+                project(banks[2][t][:], 2, t, a)
+        best = merge(2, best, "best2")
+
+        last = []
+        for ch in range(CHUNKS):
+            bank = psum.tile([P, 4, CHUNK], F32, name=f"a3_{ch}", tag=f"bank1{ch}")
+            for t in range(4):
+                for a in range(PASSES):
+                    project(bank[:, t, :], 3, t, a, ch * CHUNK, CHUNK)
+            last.append(bank)
 
         wc_bytes = wc_codes[:].bitcast(U8)
         wc_scale_bytes = wc_planes[:].bitcast(U8)
-        h_bf = []
-        for ch in range(CHUNKS):
+        wd_tag = {1: "c_bf0"}
+        out_rows = out.rearrange("(u p) j -> p u j", p=P)
+        own, pooled, h_bf, ys = {}, {}, {}, {}
+
+        def project_own(ch):
             half, x0 = divmod(ch * CHUNK, HALF)
-            own = psum.tile([P, 4, CHUNK], F32, name=f"own{ch}", tag="bank")
+            own[ch] = psum.tile([P, 4, CHUNK], F32, name=f"own{ch}", tag=f"bank0{ch}")
             for t in range(4):
                 for a in range(PASSES):
                     nc.tensor.matmul_mx(
-                        out=own[:, t, :],
+                        out=own[ch][:, t, :],
                         lhsT=wc_bytes[:, a, 2 * t * P : 2 * (t + 1) * P].bitcast(FP4X4),
                         lhsT_scale=wc_scale_bytes[:, a, t * P : (t + 1) * P],
                         rhs=c_codes[:, half, a, x0 : x0 + CHUNK].bitcast(FP8X4),
@@ -218,35 +240,35 @@ def tile_list_pnet_gate_kernel(
                         start=(a == 0),
                         stop=(a == PASSES - 1),
                     )
-            summed = keep.tile([P, 4, CHUNK], F32, name=f"summed{ch}")
-            nc.vector.tensor_tensor(summed[:], own[:], best[:, :, ch * CHUNK : (ch + 1) * CHUNK], ALU.add)
-            if ch == 1:
-                nc.vector.quantize_mx(wd_codes[:].bitcast(FP8X4), wd_scales[:], wd_bf[:])
-            hb = keep.tile([P, CHUNK * PACK], BF16, name=f"h_bf{ch}", align_bytes=64)
+
+        def pool_last(ch):
+            pooled[ch] = keep.tile(
+                [P, 4, CHUNK], F32, name=f"pooled{ch}", tag=wd_tag.get(ch, f"pooled{ch}"), align_bytes=64
+            )
+            nc.vector.tensor_tensor(
+                pooled[ch][:], last[ch][:], best[:, :, ch * CHUNK : (ch + 1) * CHUNK], ALU.max
+            )
+
+        def add_own(ch):
+            summed = keep.tile(
+                [P, 4, CHUNK], F32, name=f"summed{ch}", tag={1: "c_bf1", 2: "wd_bf"}.get(ch, f"summed{ch}"), align_bytes=64
+            )
+            nc.vector.tensor_tensor(summed[:], own[ch][:], pooled[ch][:], ALU.add)
+            h_bf[ch] = keep.tile([P, CHUNK * PACK], BF16, name=f"h_bf{ch}", tag=("table" if ch == 0 else f"h_bf{ch}"), align_bytes=64)
             nc.scalar.activation(
-                hb[:].rearrange("p (x i t) -> p x t i", i=4, t=PACK),
+                h_bf[ch][:].rearrange("p (x i t) -> p x t i", i=4, t=PACK),
                 summed[:].rearrange("p t (x i) -> p x t i", i=4),
                 ACT.Relu,
             )
-            h_bf.append(hb)
 
-        out_rows = out.rearrange("(u p) j -> p u j", p=P)
-        ys = []
-
-        def finish(ch):
-            cols = slice(ch * CHUNK, (ch + 1) * CHUNK)
-            res = keep.tile([P, 4, CHUNK], F32, name=f"res{ch}")
-            nc.vector.tensor_tensor(res[:], ys[ch][:], gate[:, :, cols], ALU.mult)
-            nc.sync.dma_start(out_rows[:, :, cols], res[:])
-
-        for ch in range(CHUNKS):
+        def second_layer(ch):
             h_codes = keep.tile([P, CHUNK], U32, name=f"h_codes{ch}", align_bytes=64)
             h_scales = keep.tile([P, CHUNK], U8, name=f"h_scales{ch}", align_bytes=64)
             nc.vector.quantize_mx(h_codes[:].bitcast(FP8X4), h_scales[:], h_bf[ch][:])
-            y = psum.tile([P, 4, CHUNK], F32, name=f"y{ch}", tag="bank")
+            ys[ch] = psum.tile([P, 4, CHUNK], F32, name=f"y{ch}", tag=f"bank1{ch}")
             for u in range(4):
                 nc.tensor.matmul_mx(
-                    out=y[:, u, :],
+                    out=ys[ch][:, u, :],
                     lhsT=wd_codes[:, u * P : (u + 1) * P].bitcast(FP8X4),
                     lhsT_scale=wd_scales[:, u * P : (u + 1) * P],
                     rhs=h_codes[:].bitcast(FP8X4),
@@ -254,7 +276,35 @@ def tile_list_pnet_gate_kernel(
                     start=True,
                     stop=True,
                 )
-            ys.append(y)
-            if ch > 0:
-                finish(ch - 1)
-        finish(CHUNKS - 1)
+
+        def finish(ch):
+            cols = slice(ch * CHUNK, (ch + 1) * CHUNK)
+            res = keep.tile([P, 4, CHUNK], F32, name=f"res{ch}")
+            step = 2 if ch == CHUNKS - 1 else 4
+            for u in range(0, 4, step):
+                us = slice(u, u + step)
+                nc.vector.tensor_tensor(res[:, us, :], ys[ch][:, us, :], gate[:, us, cols], ALU.mult)
+                nc.sync.dma_start(out_rows[:, us, cols], res[:, us, :])
+
+        project_own(0)
+        project_own(1)
+        pool_last(0)
+        pool_last(1)
+        quantize_c(1)
+        project_own(2)
+        project_own(3)
+        add_own(0)
+        pool_last(2)
+        add_own(1)
+        nc.vector.quantize_mx(wd_codes[:].bitcast(FP8X4), wd_scales[:], wd_bf[:])
+        second_layer(0)
+        add_own(2)
+        second_layer(1)
+        pool_last(3)
+        finish(0)
+        add_own(3)
+        second_layer(2)
+        finish(1)
+        second_layer(3)
+        finish(2)
+        finish(3)

@@ -33,83 +33,148 @@ def tile_list_pnet_gate_kernel(
     nc = tc.nc
     with ExitStack() as ctx:
         keep = ctx.enter_context(tc.tile_pool(name="keep", bufs=1))
+        work = ctx.enter_context(tc.tile_pool(name="work", bufs=1))
         psum = ctx.enter_context(tc.psum_pool(name="psum", bufs=1))
+
+        LAP = 64
+        RAW = 4096
+        at = {}
+        at["gate"] = 0
+        at["w1b"] = at["gate"] + 8192 - LAP
+        at["rows"] = at["w1b"] + RAW - LAP
+        at["c00"] = at["rows"] + RAW - LAP
+        at["words23"] = at["rows"] - LAP
+        at["best0"] = at["c00"] + RAW
+        at["c01"] = at["best0"] + 8192 - LAP
+        at["w0a"] = at["c01"] + RAW - LAP
+        at["wc_raw"] = at["w0a"] + RAW - LAP
+        at["c10"] = at["wc_raw"] + 2048
+        at["w0b"] = at["c10"] + RAW - LAP
+        at["words1"] = at["w0b"] + LAP
+        at["wc_codes"] = at["words1"]
+        at["wcs_sorted"] = at["words1"] + 2048
+        at["picked23"] = at["w0b"] + RAW - LAP
+        at["summed1"] = at["picked23"] + 4096
+        at["c11"] = at["summed1"] + 2048 - LAP
+        at["summed0"] = at["c11"] + LAP
+        at["summed3"] = at["summed0"]
+        at["w1a"] = at["c11"] + RAW - LAP
+        at["wd_raw"] = at["w1a"] + RAW - LAP
+        at["summed2"] = at["wd_raw"] + LAP
+        at["h_bf0"] = at["summed2"] + 2048
+        at["h_bf1"] = at["h_bf0"] + 1024
+        at["words0"] = at["wd_raw"] + 8192
+        at["c_bf1"] = at["words0"] + 2048 - LAP
+
+        def tile(name, shape, dtype):
+            if name in at:
+                return work.tile(shape, dtype, name=name, align_bytes=64, offset=at[name])
+            return keep.tile(shape, dtype, name=name, align_bytes=64)
 
         offsets = keep.tile([P, G * LIST_COLS], U16, name="offsets")
         nc.sync.dma_start(offsets[:], offs)
 
-        scale_rows = keep.tile([P, T // 4], I32, name="scale_rows", tag="rows", align_bytes=64)
-        nc.sync.dma_start(scale_rows[0:32, :], tab_scales.rearrange("a q t -> q a t").bitcast(I32))
-        nc.vector.memset(scale_rows[32:64, :], 0)
-        nc.vector.memset(scale_rows[64:128, :], 0)
+        scale_rows = tile("rows", [P, T // 4], I32)
+        nc.sync.dma_start(scale_rows[96:128, :], tab_scales.rearrange("a q t -> q a t").bitcast(I32))
+        nc.vector.memset(scale_rows[0:96, :], 0)
 
-        table = keep.tile([P, T], I32, name="table", tag="table", align_bytes=64)
+        table = tile("table", [P, T], I32)
         nc.sync.dma_start(table[:], tab_words[0].rearrange("p t b -> p (t b)").bitcast(I32))
 
-        def load_half(src, a, half, tag):
-            raw = keep.tile([P, PACK, HALF], F32, name="raw", tag=tag, align_bytes=64)
+        wcs_rows = tile("wcs_rows", [32, R // 4], I32)
+        nc.sync.dma_start(wcs_rows[:], wc_scales.rearrange("a q n -> q a n").bitcast(I32))
+
+        planes = tile("planes", [P, PASSES, G * J // 4], I32)
+        nc.gpsimd.memset(planes[:], 0)
+        wc_planes = tile("wc_planes", [P, PASSES, R // 4], I32)
+        nc.gpsimd.memset(wc_planes[:], 0)
+
+        def load_half(src, a, half, name):
+            raw = tile(name, [P, PACK, HALF], F32)
             rows = src[a * K_PASS : (a + 1) * K_PASS, half * HALF : (half + 1) * HALF]
             nc.sync.dma_start(raw[:], rows.rearrange("(p j) x -> p j x", j=PACK))
             return raw
 
-        w_codes = keep.tile([P, PASSES, R], U32, name="w_codes", align_bytes=64)
-        w_scales = keep.tile([P, PASSES, R], U8, name="w_scales", align_bytes=64)
-        w_bfs = []
-        for a in range(PASSES):
-            w_bf = keep.tile([P, R * PACK], BF16, name=f"w_bf{a}", tag=f"w_bf{a}", align_bytes=64)
-            dst = w_bf[:].rearrange("p (t h i j) -> p h t j i", t=4, i=4, j=PACK)
-            for half in range(2):
-                raw = load_half(w, a, half, f"stage{2 * a + half}")
-                src = raw[:].rearrange("p j (h t i) -> p h t j i", t=4, i=4)
-                part = dst[:, 16 * half : 16 * half + 16]
-                if a == 0 and half == 0:
-                    for t in range(4):
-                        nc.scalar.activation(part[:, :, t], src[:, :, t], ACT.Copy)
-                else:
-                    nc.scalar.copy(part, src)
-            w_bfs.append(w_bf)
+        w_codes = tile("w_codes", [P, PASSES, R], U32)
+        w_scales = tile("w_scales", [P, PASSES, R], U8)
+        w_bfs = [tile(f"w_bf{a}", [P, R * PACK], BF16) for a in range(PASSES)]
+
+        def cast_w(a, half):
+            raw = load_half(w, a, half, f"w{a}{'ab'[half]}")
+            dst = w_bfs[a][:].rearrange("p (t h i j) -> p h t j i", t=4, i=4, j=PACK)
+            src = raw[:].rearrange("p j (h t i) -> p h t j i", t=4, i=4)
+            part = dst[:, 16 * half : 16 * half + 16]
+            if a == 0 and half == 0:
+                nc.scalar.activation(part[:, :, 0], src[:, :, 0], ACT.Copy)
+                nc.scalar.copy(part[:, :, 1:4], src[:, :, 1:4])
+            else:
+                nc.scalar.copy(part, src)
 
         def quantize_w(a):
             nc.vector.quantize_mx(w_codes[:, a, :].bitcast(FP8X4), w_scales[:, a, :], w_bfs[a][:])
 
-        picked_scales = keep.tile([P, G * J], U8, name="picked_scales", tag="picked_scales", align_bytes=64)
+        cast_w(0, 0)
+        cast_w(0, 1)
+        cast_w(1, 0)
+
+        picked_scales = tile("picked_scales", [P, G * J], U8)
         for s in range(2):
             nc.vector.tensor_copy(
                 picked_scales[:, s * 2 * J : (s + 1) * 2 * J],
                 scale_rows[:].bitcast(U8).indirect(offsets[:, s * 2 * LIST_COLS : (s + 1) * 2 * LIST_COLS]),
             )
-        planes = keep.tile([P, PASSES, G * J // 4], I32, name="planes", align_bytes=64)
-        nc.gpsimd.memset(planes[:], 0)
         for q in range(4):
-            nc.sync.dma_start(planes[32 * q : 32 * q + 4], picked_scales[8 * q : 8 * q + 8, :].bitcast(I32))
+            nc.sync.dma_start(
+                planes[32 * q : 32 * q + 4], picked_scales[96 + 8 * q : 96 + 8 * q + 8, :].bitcast(I32)
+            )
         tab_planes = planes[:].bitcast(U8)
+        cast_w(1, 1)
+        c_raw = {(0, 0): load_half(c, 0, 0, "c00")}
+
+        c_raw[0, 1] = load_half(c, 1, 0, "c01")
+        wc_raw = tile("wc_raw", [P, PASSES, R // 2], I32)
+        nc.sync.dma_start(wc_raw[:], wc_words.rearrange("a p b -> p a b").bitcast(I32))
+        c_raw[1, 0] = load_half(c, 0, 1, "c10")
+        c_raw[1, 1] = load_half(c, 1, 1, "c11")
+        wd_raw = tile("wd_raw", [P, PACK, N], F32)
+        wd_rows = wd.rearrange("(h t i) n -> t h i n", t=4, i=4)
+        for t in range(4):
+            nc.sync.dma_start(wd_raw[:, t, :], wd_rows[t])
+        gate = tile("gate", [P, 4, J], F32)
+        nc.sync.dma_start(gate[:], gm.rearrange("(u p) j -> p u j", p=P))
 
         parted = {}
         picked = {}
 
-        def pick(g0, count, tag):
-            picked[g0] = keep.tile([P, count * J], U32, name=f"picked{g0}", tag=tag, align_bytes=64)
+        def pick(g0, count, name):
+            picked[g0] = tile(name, [P, count * J], U32)
             nc.vector.tensor_copy(
                 picked[g0][:],
                 table[:].bitcast(U32).indirect(offsets[:, g0 * LIST_COLS : (g0 + count) * LIST_COLS]),
             )
 
-        def part_passes(g0, count, tag):
-            words = keep.tile([P, PASSES, 2 * count * J], U8, name=f"words{g0}", tag=tag, align_bytes=64)
+        def part_passes(g0, count, name):
+            words = tile(name, [P, PASSES, 2 * count * J], U8)
             nc.vector.tensor_copy(
                 words[:].bitcast(U16), picked[g0][:].bitcast(U16).rearrange("p (n d) -> p d n", d=PASSES)
             )
             for k in range(count):
                 parted[g0 + k] = words[:, :, 2 * k * J : 2 * (k + 1) * J]
 
-        pick(0, 2, "picked0")
-        pick(2, 1, "picked2")
-        part_passes(0, 2, "words0")
+        pick(0, 1, "picked0")
+        pick(1, 1, "picked1")
+        part_passes(0, 1, "words0")
         quantize_w(0)
-        part_passes(2, 1, "w_bf0")
+        part_passes(1, 1, "words1")
+        wcs_sorted = tile("wcs_sorted", [32, R // 4], I32)
+        nc.vector.tensor_copy(
+            wcs_sorted[:].rearrange("p (t h) -> p t h", t=4), wcs_rows[:].rearrange("p (h t) -> p t h", t=4)
+        )
+        for q in range(4):
+            nc.sync.dma_start(wc_planes[32 * q : 32 * q + 4], wcs_sorted[8 * q : 8 * q + 8, :])
+        pick(2, 2, "picked23")
         quantize_w(1)
-        pick(3, 1, "w_bf1")
-        part_passes(3, 1, "words3")
+        part_passes(2, 2, "words23")
 
         def project(dst, g, t, a, j0=0, width=J):
             nc.tensor.matmul_mx(
@@ -126,28 +191,23 @@ def tile_list_pnet_gate_kernel(
             return [psum.tile([P, J], F32, name=f"a{g}_{t}", tag=f"bank{g % 2}{t}") for t in range(4)]
 
         banks = [new_banks(0), new_banks(1)]
+        for g in range(2):
+            for t in range(4):
+                project(banks[g][t][:], g, t, 0)
         for t in range(4):
-            project(banks[0][t][:], 0, t, 0)
-        for t in range(4):
-            project(banks[0][t][:], 0, t, 1)
-            project(banks[1][t][:], 1, t, 0)
-            project(banks[1][t][:], 1, t, 1)
+            for g in range(2):
+                project(banks[g][t][:], g, t, 1)
 
-        c_codes = keep.tile([P, 2, PASSES, HALF], U32, name="c_codes", align_bytes=64)
-        c_bfs = []
-        for half in range(2):
-            c_bf = keep.tile([P, PASSES, HALF * PACK], BF16, name=f"c_bf{half}", tag=f"c_bf{half}", align_bytes=64)
-            for a in range(PASSES):
-                raw = load_half(c, a, half, ("rows", "stage0", "stage1", "stage2")[2 * half + a])
-                nc.scalar.copy(
-                    c_bf[:, a, :].rearrange("p (x i j) -> p x j i", i=4, j=PACK),
-                    raw[:].rearrange("p j (x i) -> p x j i", i=4),
-                )
-                if (half, a) == (0, 0):
-                    best = keep.tile([P, 4, J], F32, name="best0", tag="rows", align_bytes=64)
-                    for t in range(4):
-                        nc.scalar.copy(best[:, t, :], banks[0][t][:])
-            c_bfs.append(c_bf)
+        c_codes = tile("c_codes", [P, 2, PASSES, HALF], U32)
+        c_scales = tile("c_scales", [P, 2, PASSES, HALF], U8)
+
+        def cast_c(dst, half, a):
+            nc.scalar.copy(
+                dst.rearrange("p (x i j) -> p x j i", i=4, j=PACK),
+                c_raw[half, a][:].rearrange("p j (x i) -> p x j i", i=4),
+            )
+
+        c_bfs = [tile(f"c_bf{half}", [P, PASSES, HALF * PACK], BF16) for half in range(2)]
 
         def quantize_c(half):
             nc.vector.quantize_mx(
@@ -156,65 +216,44 @@ def tile_list_pnet_gate_kernel(
                 c_bfs[half][:].rearrange("p a x -> p (a x)"),
             )
 
-        wc_raw = keep.tile([P, PASSES, R // 2], I32, name="wc_raw", tag="stage3", align_bytes=64)
-        nc.sync.dma_start(wc_raw[:], wc_words.rearrange("a p b -> p a b").bitcast(I32))
-        wc_codes = keep.tile([P, PASSES, R // 2], I32, name="wc_codes", align_bytes=64)
-
-        wd_raw = keep.tile([P, PACK, N], F32, name="wd_raw", tag="table", align_bytes=64)
-        wd_rows = wd.rearrange("(h t i) n -> t h i n", t=4, i=4)
+        for a in range(PASSES):
+            cast_c(c_bfs[0][:, a, :], 0, a)
+        quantize_c(0)
+        best = tile("best0", [P, 4, J], F32)
         for t in range(4):
-            nc.sync.dma_start(wd_raw[:, t, :], wd_rows[t])
+            nc.scalar.copy(best[:, t, :], banks[0][t][:])
+        for a in range(PASSES):
+            cast_c(c_bfs[1][:, a, :], 1, a)
 
-        wcs_raw = keep.tile([P, PASSES, R // 4], I32, name="wcs_raw", tag="picked_scales", align_bytes=64)
-        nc.gpsimd.memset(wcs_raw[:], 0)
-        for q in range(4):
-            nc.sync.dma_start(
-                wcs_raw[32 * q : 32 * q + 4],
-                wc_scales[:, 4 * q : 4 * q + 4, :].rearrange("a r n -> r a n").bitcast(I32),
-            )
-        wc_planes = keep.tile([P, PASSES, R // 4], I32, name="wc_planes", align_bytes=64)
-
-        def order_wc():
-            nc.vector.tensor_copy(
-                wc_codes[:].rearrange("p a (t h x) -> p a t h x", t=4, x=2),
-                wc_raw[:].rearrange("p a (h t x) -> p a t h x", t=4, x=2),
-            )
-            nc.vector.tensor_copy(
-                wc_planes[:].rearrange("p a (t h) -> p a t h", t=4),
-                wcs_raw[:].rearrange("p a (h t) -> p a t h", t=4),
-            )
-
-        c_scales = keep.tile([P, 2, PASSES, HALF], U8, name="c_scales", align_bytes=64)
-        wd_bf = keep.tile([P, N * PACK], BF16, name="wd_bf", tag="wd_bf", align_bytes=64)
+        wd_bf = tile("wd_bf", [P, N * PACK], BF16)
         nc.scalar.copy(
             wd_bf[:].rearrange("p (x i t) -> p x t i", i=4, t=PACK),
             wd_raw[:].rearrange("p t (x i) -> p x t i", i=4),
         )
-        wd_codes = keep.tile([P, N], U32, name="wd_codes", align_bytes=64)
-        wd_scales = keep.tile([P, N], U8, name="wd_scales", align_bytes=64)
+        wd_codes = tile("wd_codes", [P, N], U32)
+        wd_scales = tile("wd_scales", [P, N], U8)
 
-        gate = keep.tile([P, 4, J], F32, name="gate", tag="stage1", align_bytes=64)
-        nc.sync.dma_start(gate[:], gm.rearrange("(u p) j -> p u j", p=P))
-
-        def merge(g, best, tag):
-            merged = keep.tile([P, 4, J], F32, name=f"best{g}", tag=tag, align_bytes=64)
+        def merge(g, best):
+            merged = tile(f"best{g}", [P, 4, J], F32)
             for t in range(4):
-                if (g, t) == (2, 2):
-                    quantize_c(0)
                 nc.vector.tensor_tensor(merged[:, t, :], banks[g][t][:], best[:, t, :], ALU.max)
             return merged
 
-        best = merge(1, best, "best1")
-        order_wc()
+        best = merge(1, best)
+        wc_codes = tile("wc_codes", [P, PASSES, R // 2], I32)
+        nc.vector.tensor_copy(
+            wc_codes[:].rearrange("p a (t h x) -> p a t h x", t=4, x=2),
+            wc_raw[:].rearrange("p a (h t x) -> p a t h x", t=4, x=2),
+        )
         banks.append(new_banks(2))
         for t in range(4):
             for a in range(PASSES):
                 project(banks[2][t][:], 2, t, a)
-        best = merge(2, best, "best2")
+        best = merge(2, best)
 
         last = []
         for ch in range(CHUNKS):
-            bank = psum.tile([P, 4, CHUNK], F32, name=f"a3_{ch}", tag=f"bank1{ch}")
+            bank = psum.tile([P, 4, CHUNK], F32, name=f"a3_{ch}", tag=("bank10", "bank11", "bank02", "bank03")[ch])
             for t in range(4):
                 for a in range(PASSES):
                     project(bank[:, t, :], 3, t, a, ch * CHUNK, CHUNK)
@@ -222,13 +261,12 @@ def tile_list_pnet_gate_kernel(
 
         wc_bytes = wc_codes[:].bitcast(U8)
         wc_scale_bytes = wc_planes[:].bitcast(U8)
-        wd_tag = {1: "c_bf0"}
         out_rows = out.rearrange("(u p) j -> p u j", p=P)
         own, pooled, h_bf, ys = {}, {}, {}, {}
 
         def project_own(ch):
             half, x0 = divmod(ch * CHUNK, HALF)
-            own[ch] = psum.tile([P, 4, CHUNK], F32, name=f"own{ch}", tag=f"bank0{ch}")
+            own[ch] = psum.tile([P, 4, CHUNK], F32, name=f"own{ch}", tag=("bank12", "bank13", "bank02", "bank03")[ch])
             for t in range(4):
                 for a in range(PASSES):
                     nc.tensor.matmul_mx(
@@ -242,19 +280,15 @@ def tile_list_pnet_gate_kernel(
                     )
 
         def pool_last(ch):
-            pooled[ch] = keep.tile(
-                [P, 4, CHUNK], F32, name=f"pooled{ch}", tag=wd_tag.get(ch, f"pooled{ch}"), align_bytes=64
-            )
+            pooled[ch] = tile(f"pooled{ch}", [P, 4, CHUNK], F32)
             nc.vector.tensor_tensor(
                 pooled[ch][:], last[ch][:], best[:, :, ch * CHUNK : (ch + 1) * CHUNK], ALU.max
             )
 
         def add_own(ch):
-            summed = keep.tile(
-                [P, 4, CHUNK], F32, name=f"summed{ch}", tag={1: "c_bf1", 2: "wd_bf"}.get(ch, f"summed{ch}"), align_bytes=64
-            )
+            summed = tile(f"summed{ch}", [P, 4, CHUNK], F32)
             nc.vector.tensor_tensor(summed[:], own[ch][:], pooled[ch][:], ALU.add)
-            h_bf[ch] = keep.tile([P, CHUNK * PACK], BF16, name=f"h_bf{ch}", tag=("table" if ch == 0 else f"h_bf{ch}"), align_bytes=64)
+            h_bf[ch] = tile(f"h_bf{ch}", [P, CHUNK * PACK], BF16)
             nc.scalar.activation(
                 h_bf[ch][:].rearrange("p (x i t) -> p x t i", i=4, t=PACK),
                 summed[:].rearrange("p t (x i) -> p x t i", i=4),
@@ -265,7 +299,7 @@ def tile_list_pnet_gate_kernel(
             h_codes = keep.tile([P, CHUNK], U32, name=f"h_codes{ch}", align_bytes=64)
             h_scales = keep.tile([P, CHUNK], U8, name=f"h_scales{ch}", align_bytes=64)
             nc.vector.quantize_mx(h_codes[:].bitcast(FP8X4), h_scales[:], h_bf[ch][:])
-            ys[ch] = psum.tile([P, 4, CHUNK], F32, name=f"y{ch}", tag=f"bank1{ch}")
+            ys[ch] = psum.tile([P, 4, CHUNK], F32, name=f"y{ch}", tag=("bank00", "bank01", "bank10", "bank11")[ch])
             for u in range(4):
                 nc.tensor.matmul_mx(
                     out=ys[ch][:, u, :],
@@ -291,20 +325,20 @@ def tile_list_pnet_gate_kernel(
         pool_last(0)
         pool_last(1)
         quantize_c(1)
-        project_own(2)
-        project_own(3)
-        add_own(0)
         pool_last(2)
+        project_own(2)
+        add_own(0)
+        pool_last(3)
+        project_own(3)
         add_own(1)
         nc.vector.quantize_mx(wd_codes[:].bitcast(FP8X4), wd_scales[:], wd_bf[:])
-        second_layer(0)
         add_own(2)
-        second_layer(1)
-        pool_last(3)
-        finish(0)
+        second_layer(0)
         add_own(3)
+        second_layer(1)
         second_layer(2)
-        finish(1)
+        finish(0)
         second_layer(3)
+        finish(1)
         finish(2)
         finish(3)

@@ -50,9 +50,9 @@ def tile_list_pnet_gate_kernel(
         at["wc_raw"] = at["w0a"] + RAW - LAP
         at["c10"] = at["wc_raw"] + 2048
         at["w0b"] = at["c10"] + RAW - LAP
-        at["words1"] = at["w0b"] + LAP
+        at["words1"] = at["w1b"] + LAP
         at["wc_codes"] = at["words1"]
-        at["wcs_sorted"] = at["words1"] + 2048
+        at["wcs_sorted"] = at["w0b"] + LAP
         at["picked23"] = at["w0b"] + RAW - LAP
         at["summed1"] = at["picked23"] + 4096
         at["c11"] = at["summed1"] + 2048 - LAP
@@ -165,15 +165,15 @@ def tile_list_pnet_gate_kernel(
         pick(1, 1, "picked1")
         part_passes(0, 1, "words0")
         quantize_w(0)
-        part_passes(1, 1, "words1")
+        pick(2, 2, "picked23")
         wcs_sorted = tile("wcs_sorted", [32, R // 4], I32)
         nc.vector.tensor_copy(
             wcs_sorted[:].rearrange("p (t h) -> p t h", t=4), wcs_rows[:].rearrange("p (h t) -> p t h", t=4)
         )
         for q in range(4):
             nc.sync.dma_start(wc_planes[32 * q : 32 * q + 4], wcs_sorted[8 * q : 8 * q + 8, :])
-        pick(2, 2, "picked23")
         quantize_w(1)
+        part_passes(1, 1, "words1")
         part_passes(2, 2, "words23")
 
         def project(dst, g, t, a, j0=0, width=J):
@@ -191,12 +191,12 @@ def tile_list_pnet_gate_kernel(
             return [psum.tile([P, J], F32, name=f"a{g}_{t}", tag=f"bank{g % 2}{t}") for t in range(4)]
 
         banks = [new_banks(0), new_banks(1)]
-        for g in range(2):
+        for a in range(PASSES):
             for t in range(4):
-                project(banks[g][t][:], g, t, 0)
+                project(banks[0][t][:], 0, t, a)
         for t in range(4):
-            for g in range(2):
-                project(banks[g][t][:], g, t, 1)
+            for a in range(PASSES):
+                project(banks[1][t][:], 1, t, a)
 
         c_codes = tile("c_codes", [P, 2, PASSES, HALF], U32)
         c_scales = tile("c_scales", [P, 2, PASSES, HALF], U8)

@@ -51,20 +51,26 @@ def tile_list_pnet_gate_kernel(
         at["c10"] = at["wc_raw"] + 2048
         at["w0b"] = at["c10"] + RAW - LAP
         at["words1"] = at["w1b"] + LAP
-        at["wc_codes"] = at["words1"]
-        at["wcs_sorted"] = at["w0b"] + LAP
         at["picked23"] = at["w0b"] + RAW - LAP
-        at["summed1"] = at["picked23"] + 4096
-        at["c11"] = at["summed1"] + 2048 - LAP
-        at["summed0"] = at["c11"] + LAP
-        at["summed3"] = at["summed0"]
+        at["c11"] = at["picked23"] + 4096
         at["w1a"] = at["c11"] + RAW - LAP
         at["wd_raw"] = at["w1a"] + RAW - LAP
-        at["summed2"] = at["wd_raw"] + LAP
-        at["h_bf0"] = at["summed2"] + 2048
+        at["h_bf0"] = at["wd_raw"] + LAP
         at["h_bf1"] = at["h_bf0"] + 1024
         at["words0"] = at["wd_raw"] + 8192
         at["c_bf1"] = at["words0"] + 2048 - LAP
+        at["mid2"] = at["c_bf1"]
+        at["mid3"] = at["c_bf1"] + 2048
+        at["pooled0"] = at["c11"] + LAP - 2048
+        at["own_sb0"] = at["c11"] + LAP
+        at["own_sb1"] = at["own_sb0"] + 2048
+        at["wd_codes"] = at["own_sb1"]
+        at["pooled1"] = at["mid3"] + 2048
+        at["mid0"] = at["pooled1"] + 2048 - LAP
+        at["wd_bf0"] = at["mid0"] + LAP
+        at["c_codes0"] = at["wd_bf0"] + 2048
+        at["wd_bf1"] = at["c_codes0"]
+        at["summed2"] = at["wd_bf1"]
 
         def tile(name, shape, dtype):
             if name in at:
@@ -131,6 +137,12 @@ def tile_list_pnet_gate_kernel(
         cast_w(1, 1)
         c_raw = {(0, 0): load_half(c, 0, 0, "c00")}
 
+        wcs_sorted = tile("wcs_sorted", [32, R // 4], I32)
+        nc.vector.tensor_copy(
+            wcs_sorted[:].rearrange("p (t h) -> p t h", t=4), wcs_rows[:].rearrange("p (h t) -> p t h", t=4)
+        )
+        for q in range(4):
+            nc.sync.dma_start(wc_planes[32 * q : 32 * q + 4], wcs_sorted[8 * q : 8 * q + 8, :])
         c_raw[0, 1] = load_half(c, 1, 0, "c01")
         wc_raw = tile("wc_raw", [P, PASSES, R // 2], I32)
         nc.sync.dma_start(wc_raw[:], wc_words.rearrange("a p b -> p a b").bitcast(I32))
@@ -166,12 +178,6 @@ def tile_list_pnet_gate_kernel(
         part_passes(0, 1, "words0")
         quantize_w(0)
         pick(2, 2, "picked23")
-        wcs_sorted = tile("wcs_sorted", [32, R // 4], I32)
-        nc.vector.tensor_copy(
-            wcs_sorted[:].rearrange("p (t h) -> p t h", t=4), wcs_rows[:].rearrange("p (h t) -> p t h", t=4)
-        )
-        for q in range(4):
-            nc.sync.dma_start(wc_planes[32 * q : 32 * q + 4], wcs_sorted[8 * q : 8 * q + 8, :])
         quantize_w(1)
         part_passes(1, 1, "words1")
         part_passes(2, 2, "words23")
@@ -198,7 +204,7 @@ def tile_list_pnet_gate_kernel(
             for a in range(PASSES):
                 project(banks[1][t][:], 1, t, a)
 
-        c_codes = tile("c_codes", [P, 2, PASSES, HALF], U32)
+        c_codes = {}
         c_scales = tile("c_scales", [P, 2, PASSES, HALF], U8)
 
         def cast_c(dst, half, a):
@@ -210,8 +216,9 @@ def tile_list_pnet_gate_kernel(
         c_bfs = [tile(f"c_bf{half}", [P, PASSES, HALF * PACK], BF16) for half in range(2)]
 
         def quantize_c(half):
+            c_codes[half] = tile(f"c_codes{half}", [P, PASSES, HALF], U32)
             nc.vector.quantize_mx(
-                c_codes[:, half].rearrange("p a x -> p (a x)").bitcast(FP8X4),
+                c_codes[half][:].rearrange("p a x -> p (a x)").bitcast(FP8X4),
                 c_scales[:, half].rearrange("p a x -> p (a x)"),
                 c_bfs[half][:].rearrange("p a x -> p (a x)"),
             )
@@ -225,69 +232,66 @@ def tile_list_pnet_gate_kernel(
         for a in range(PASSES):
             cast_c(c_bfs[1][:, a, :], 1, a)
 
-        wd_bf = tile("wd_bf", [P, N * PACK], BF16)
-        nc.scalar.copy(
-            wd_bf[:].rearrange("p (x i t) -> p x t i", i=4, t=PACK),
-            wd_raw[:].rearrange("p t (x i) -> p x t i", i=4),
-        )
-        wd_codes = tile("wd_codes", [P, N], U32)
-        wd_scales = tile("wd_scales", [P, N], U8)
-
-        def merge(g, best):
-            merged = tile(f"best{g}", [P, 4, J], F32)
-            for t in range(4):
-                nc.vector.tensor_tensor(merged[:, t, :], banks[g][t][:], best[:, t, :], ALU.max)
-            return merged
-
-        best = merge(1, best)
         wc_codes = tile("wc_codes", [P, PASSES, R // 2], I32)
         nc.vector.tensor_copy(
             wc_codes[:].rearrange("p a (t h x) -> p a t h x", t=4, x=2),
             wc_raw[:].rearrange("p a (h t x) -> p a t h x", t=4, x=2),
         )
-        banks.append(new_banks(2))
+        best1 = tile("best1", [P, 4, J], F32)
         for t in range(4):
-            for a in range(PASSES):
-                project(banks[2][t][:], 2, t, a)
-        best = merge(2, best)
+            nc.vector.tensor_tensor(best1[:, t, :], banks[1][t][:], best[:, t, :], ALU.max)
 
-        last = []
-        for ch in range(CHUNKS):
-            bank = psum.tile([P, 4, CHUNK], F32, name=f"a3_{ch}", tag=("bank10", "bank11", "bank02", "bank03")[ch])
+        late = {}
+
+        def project_late(g, ch, tag):
+            bank = psum.tile([P, 4, CHUNK], F32, name=f"a{g}_{ch}", tag=tag)
             for t in range(4):
                 for a in range(PASSES):
-                    project(bank[:, t, :], 3, t, a, ch * CHUNK, CHUNK)
-            last.append(bank)
+                    project(bank[:, t, :], g, t, a, ch * CHUNK, CHUNK)
+            late[g, ch] = bank
 
         wc_bytes = wc_codes[:].bitcast(U8)
         wc_scale_bytes = wc_planes[:].bitcast(U8)
         out_rows = out.rearrange("(u p) j -> p u j", p=P)
         own, pooled, h_bf, ys = {}, {}, {}, {}
 
-        def project_own(ch):
+        def project_own(ch, tag):
             half, x0 = divmod(ch * CHUNK, HALF)
-            own[ch] = psum.tile([P, 4, CHUNK], F32, name=f"own{ch}", tag=("bank12", "bank13", "bank02", "bank03")[ch])
+            own[ch] = psum.tile([P, 4, CHUNK], F32, name=f"own{ch}", tag=tag)
             for t in range(4):
                 for a in range(PASSES):
                     nc.tensor.matmul_mx(
                         out=own[ch][:, t, :],
                         lhsT=wc_bytes[:, a, 2 * t * P : 2 * (t + 1) * P].bitcast(FP4X4),
                         lhsT_scale=wc_scale_bytes[:, a, t * P : (t + 1) * P],
-                        rhs=c_codes[:, half, a, x0 : x0 + CHUNK].bitcast(FP8X4),
+                        rhs=c_codes[half][:, a, x0 : x0 + CHUNK].bitcast(FP8X4),
                         rhs_scale=c_scales[:, half, a, x0 : x0 + CHUNK],
                         start=(a == 0),
                         stop=(a == PASSES - 1),
                     )
 
+        mid, own_sb = {}, {}
+
+        def pool_mid(ch):
+            mid[ch] = tile(f"mid{ch}", [P, 4, CHUNK], F32)
+            nc.vector.tensor_tensor(
+                mid[ch][:], late[2, ch][:], best1[:, :, ch * CHUNK : (ch + 1) * CHUNK], ALU.max
+            )
+
         def pool_last(ch):
             pooled[ch] = tile(f"pooled{ch}", [P, 4, CHUNK], F32)
-            nc.vector.tensor_tensor(
-                pooled[ch][:], last[ch][:], best[:, :, ch * CHUNK : (ch + 1) * CHUNK], ALU.max
-            )
+            nc.vector.tensor_tensor(pooled[ch][:], late[3, ch][:], mid[ch][:], ALU.max)
+
+        def copy_own(ch):
+            own_sb[ch] = tile(f"own_sb{ch}", [P, 4, CHUNK], F32)
+            nc.scalar.copy(own_sb[ch][:], own[ch][:])
 
         def add_own(ch):
             summed = tile(f"summed{ch}", [P, 4, CHUNK], F32)
-            nc.vector.tensor_tensor(summed[:], own[ch][:], pooled[ch][:], ALU.add)
+            if ch < 2:
+                nc.gpsimd.tensor_tensor(summed[:], own_sb[ch][:], pooled[ch][:], ALU.add)
+            else:
+                nc.vector.tensor_tensor(summed[:], own[ch][:], pooled[ch][:], ALU.add)
             h_bf[ch] = tile(f"h_bf{ch}", [P, CHUNK * PACK], BF16)
             nc.scalar.activation(
                 h_bf[ch][:].rearrange("p (x i t) -> p x t i", i=4, t=PACK),
@@ -299,11 +303,11 @@ def tile_list_pnet_gate_kernel(
             h_codes = keep.tile([P, CHUNK], U32, name=f"h_codes{ch}", align_bytes=64)
             h_scales = keep.tile([P, CHUNK], U8, name=f"h_scales{ch}", align_bytes=64)
             nc.vector.quantize_mx(h_codes[:].bitcast(FP8X4), h_scales[:], h_bf[ch][:])
-            ys[ch] = psum.tile([P, 4, CHUNK], F32, name=f"y{ch}", tag=("bank00", "bank01", "bank10", "bank11")[ch])
+            ys[ch] = psum.tile([P, 4, CHUNK], F32, name=f"y{ch}", tag=f"bank1{ch}")
             for u in range(4):
                 nc.tensor.matmul_mx(
                     out=ys[ch][:, u, :],
-                    lhsT=wd_codes[:, u * P : (u + 1) * P].bitcast(FP8X4),
+                    lhsT=wd_q[0][:, u * P : (u + 1) * P].bitcast(FP8X4),
                     lhsT_scale=wd_scales[:, u * P : (u + 1) * P],
                     rhs=h_codes[:].bitcast(FP8X4),
                     rhs_scale=h_scales[:],
@@ -320,25 +324,54 @@ def tile_list_pnet_gate_kernel(
                 nc.vector.tensor_tensor(res[:, us, :], ys[ch][:, us, :], gate[:, us, cols], ALU.mult)
                 nc.sync.dma_start(out_rows[:, us, cols], res[:, us, :])
 
-        project_own(0)
-        project_own(1)
-        pool_last(0)
-        pool_last(1)
+        project_late(2, 0, "bank00")
+        project_late(2, 1, "bank01")
+        project_late(3, 0, "bank02")
+        project_own(0, "bank03")
+        copy_own(0)
+        project_late(2, 2, "bank10")
+        project_late(3, 1, "bank11")
+        project_own(1, "bank12")
+        copy_own(1)
+        project_late(2, 3, "bank13")
+        wd_bf = {}
+
+        def cast_wd(half):
+            wd_bf[half] = tile(f"wd_bf{half}", [P, HALF * PACK], BF16)
+            nc.scalar.copy(
+                wd_bf[half][:].rearrange("p (x i t) -> p x t i", i=4, t=PACK),
+                wd_raw[:, :, half * HALF : (half + 1) * HALF].rearrange("p t (x i) -> p x t i", i=4),
+            )
+
+        pool_mid(0)
+        project_late(3, 2, "bank00")
+        pool_mid(1)
+        project_late(3, 3, "bank01")
         quantize_c(1)
-        pool_last(2)
-        project_own(2)
+        pool_last(0)
+        project_own(2, "bank02")
+        project_own(3, "bank03")
+        cast_wd(0)
+        cast_wd(1)
         add_own(0)
-        pool_last(3)
-        project_own(3)
+        pool_mid(2)
+        pool_last(1)
         add_own(1)
-        nc.vector.quantize_mx(wd_codes[:].bitcast(FP8X4), wd_scales[:], wd_bf[:])
-        add_own(2)
+        pool_mid(3)
+        pool_last(2)
+        pool_last(3)
+        wd_q = [tile("wd_codes", [P, N], U32)]
+        wd_scales = tile("wd_scales", [P, N], U8)
+        for half in range(2):
+            cols = slice(half * HALF, (half + 1) * HALF)
+            nc.vector.quantize_mx(wd_q[0][:, cols].bitcast(FP8X4), wd_scales[:, cols], wd_bf[half][:])
         second_layer(0)
+        add_own(2)
         add_own(3)
         second_layer(1)
-        second_layer(2)
         finish(0)
-        second_layer(3)
+        second_layer(2)
         finish(1)
+        second_layer(3)
         finish(2)
         finish(3)

@@ -39,25 +39,26 @@ def tile_list_pnet_gate_kernel(
         LAP = 64
         RAW = 4096
         at = {}
-        at["gate"] = 0
-        at["w1b"] = at["gate"] + 8192 - LAP
-        at["rows"] = at["w1b"] + RAW - LAP
-        at["c00"] = at["rows"] + RAW - LAP
-        at["words23"] = at["rows"] - LAP
-        at["best0"] = at["c00"] + RAW
-        at["c01"] = at["best0"] + 8192 - LAP
-        at["w0a"] = at["c01"] + RAW - LAP
-        at["wc_raw"] = at["w0a"] + RAW - LAP
-        at["c10"] = at["wc_raw"] + 2048
-        at["w0b"] = at["c10"] + RAW - LAP
-        at["words1"] = at["w1b"] + LAP
-        at["picked23"] = at["w0b"] + RAW - LAP
-        at["c11"] = at["picked23"] + 4096
-        at["w1a"] = at["c11"] + RAW - LAP
-        at["wd_raw"] = at["w1a"] + RAW - LAP
+        at["wd_raw"] = 0
         at["h_bf0"] = at["wd_raw"] + LAP
         at["h_bf1"] = at["h_bf0"] + 1024
-        at["words0"] = at["wd_raw"] + 8192
+        at["w1b"] = at["wd_raw"] + 8192 - LAP
+        at["words1"] = at["w1b"] + LAP
+        at["words23"] = at["w1b"] + RAW - LAP
+        at["rows"] = at["w1b"] + RAW
+        at["c00"] = at["rows"] + RAW - LAP
+        at["gate"] = at["c00"] + RAW - LAP
+        at["best0"] = at["gate"] + 8192
+        at["c01"] = at["best0"] + 8192 - LAP
+        at["w0a"] = at["c01"] + RAW - LAP
+        at["late_rows"] = at["w0a"] + LAP
+        at["wc_raw"] = at["w0a"] + RAW - LAP
+        at["w0b"] = at["wc_raw"] + 2048
+        at["picked23"] = at["w0b"] + RAW - LAP
+        at["c10"] = at["picked23"] + 4096
+        at["w1a"] = at["c10"] + RAW - LAP
+        at["c11"] = at["w1a"] + RAW - LAP
+        at["words0"] = at["c11"] + RAW + LAP
         at["c_bf1"] = at["words0"] + 2048 - LAP
         at["mid2"] = at["c_bf1"]
         at["mid3"] = at["c_bf1"] + 2048
@@ -70,7 +71,7 @@ def tile_list_pnet_gate_kernel(
         at["wd_bf0"] = at["mid0"] + LAP
         at["c_codes0"] = at["wd_bf0"] + 2048
         at["wd_bf1"] = at["c_codes0"]
-        at["summed2"] = at["wd_bf1"]
+        at["summed3"] = at["wd_bf1"]
 
         def tile(name, shape, dtype):
             if name in at:
@@ -87,13 +88,13 @@ def tile_list_pnet_gate_kernel(
         table = tile("table", [P, T], I32)
         nc.sync.dma_start(table[:], tab_words[0].rearrange("p t b -> p (t b)").bitcast(I32))
 
-        wcs_rows = tile("wcs_rows", [32, R // 4], I32)
-        nc.sync.dma_start(wcs_rows[:], wc_scales.rearrange("a q n -> q a n").bitcast(I32))
+        wcs_rows = tile("wcs_rows", [P, R // 4], I32)
+        nc.sync.dma_start(wcs_rows[96:128, :], wc_scales.rearrange("a q n -> q a n").bitcast(I32))
 
-        planes = tile("planes", [P, PASSES, G * J // 4], I32)
-        nc.gpsimd.memset(planes[:], 0)
-        wc_planes = tile("wc_planes", [P, PASSES, R // 4], I32)
-        nc.gpsimd.memset(wc_planes[:], 0)
+        early_planes = tile("early_planes", [P, PASSES, 2 * J // 4], I32)
+        nc.gpsimd.memset(early_planes[:], 0)
+        late_planes = tile("late_planes", [P, PASSES, (2 * J + R) // 4], I32)
+        nc.gpsimd.memset(late_planes[:], 0)
 
         def load_half(src, a, half, name):
             raw = tile(name, [P, PACK, HALF], F32)
@@ -122,30 +123,33 @@ def tile_list_pnet_gate_kernel(
         cast_w(0, 0)
         cast_w(0, 1)
         cast_w(1, 0)
+        cast_w(1, 1)
 
-        picked_scales = tile("picked_scales", [P, G * J], U8)
+        picked_scales = []
         for s in range(2):
+            picked_scales.append(tile(f"picked_scales{s}", [P, 2 * J], U8))
             nc.vector.tensor_copy(
-                picked_scales[:, s * 2 * J : (s + 1) * 2 * J],
+                picked_scales[s][:],
                 scale_rows[:].bitcast(U8).indirect(offsets[:, s * 2 * LIST_COLS : (s + 1) * 2 * LIST_COLS]),
             )
-        for q in range(4):
-            nc.sync.dma_start(
-                planes[32 * q : 32 * q + 4], picked_scales[96 + 8 * q : 96 + 8 * q + 8, :].bitcast(I32)
-            )
-        tab_planes = planes[:].bitcast(U8)
-        cast_w(1, 1)
-        c_raw = {(0, 0): load_half(c, 0, 0, "c00")}
 
-        wcs_sorted = tile("wcs_sorted", [32, R // 4], I32)
-        nc.vector.tensor_copy(
-            wcs_sorted[:].rearrange("p (t h) -> p t h", t=4), wcs_rows[:].rearrange("p (h t) -> p t h", t=4)
-        )
-        for q in range(4):
-            nc.sync.dma_start(wc_planes[32 * q : 32 * q + 4], wcs_sorted[8 * q : 8 * q + 8, :])
+        def move_rows(planes, rows):
+            for q in (0, 2, 1, 3):
+                nc.sync.dma_start(planes[32 * q : 32 * q + 4], rows[96 + 8 * q : 96 + 8 * q + 8, :])
+
+        move_rows(early_planes, picked_scales[0][:].bitcast(I32))
+        c_raw = {(0, 0): load_half(c, 0, 0, "c00")}
         c_raw[0, 1] = load_half(c, 1, 0, "c01")
         wc_raw = tile("wc_raw", [P, PASSES, R // 2], I32)
         nc.sync.dma_start(wc_raw[:], wc_words.rearrange("a p b -> p a b").bitcast(I32))
+        late_rows = tile("late_rows", [P, (2 * J + R) // 4], I32)
+        nc.vector.tensor_copy(late_rows[96:128, 0 : 2 * J // 4], picked_scales[1][96:128, :].bitcast(I32))
+        nc.vector.tensor_copy(
+            late_rows[96:128, 2 * J // 4 :].rearrange("p (t h) -> p t h", t=4),
+            wcs_rows[96:128, :].rearrange("p (h t) -> p t h", t=4),
+        )
+        move_rows(late_planes, late_rows)
+        tab_planes = [early_planes[:].bitcast(U8), late_planes[:].bitcast(U8)]
         c_raw[1, 0] = load_half(c, 0, 1, "c10")
         c_raw[1, 1] = load_half(c, 1, 1, "c11")
         wd_raw = tile("wd_raw", [P, PACK, N], F32)
@@ -188,7 +192,7 @@ def tile_list_pnet_gate_kernel(
                 lhsT=w_codes[:, a, t * P : (t + 1) * P].bitcast(FP8X4),
                 lhsT_scale=w_scales[:, a, t * P : (t + 1) * P],
                 rhs=parted[g][:, a, 2 * j0 : 2 * (j0 + width)].bitcast(FP4X4),
-                rhs_scale=tab_planes[:, a, g * J + j0 : g * J + j0 + width],
+                rhs_scale=tab_planes[g // 2][:, a, g % 2 * J + j0 : g % 2 * J + j0 + width],
                 start=(a == 0),
                 stop=(a == PASSES - 1),
             )
@@ -251,7 +255,7 @@ def tile_list_pnet_gate_kernel(
             late[g, ch] = bank
 
         wc_bytes = wc_codes[:].bitcast(U8)
-        wc_scale_bytes = wc_planes[:].bitcast(U8)
+        wc_scale_bytes = tab_planes[1][:, :, 2 * J :]
         out_rows = out.rearrange("(u p) j -> p u j", p=P)
         own, pooled, h_bf, ys = {}, {}, {}, {}
 
@@ -360,13 +364,13 @@ def tile_list_pnet_gate_kernel(
         pool_mid(3)
         pool_last(2)
         pool_last(3)
+        add_own(2)
         wd_q = [tile("wd_codes", [P, N], U32)]
         wd_scales = tile("wd_scales", [P, N], U8)
         for half in range(2):
             cols = slice(half * HALF, (half + 1) * HALF)
             nc.vector.quantize_mx(wd_q[0][:, cols].bitcast(FP8X4), wd_scales[:, cols], wd_bf[half][:])
         second_layer(0)
-        add_own(2)
         add_own(3)
         second_layer(1)
         finish(0)

@@ -39,26 +39,26 @@ def tile_list_pnet_gate_kernel(
         LAP = 64
         RAW = 4096
         at = {}
-        at["wd_raw"] = 0
+        at["gate"] = 0
+        at["c10"] = at["gate"] + 8192 - LAP
+        at["w1a"] = at["c10"] + RAW - LAP
+        at["rows"] = at["w1a"] + RAW - LAP
+        at["c11"] = at["rows"]
+        at["w1b"] = at["rows"] + RAW - LAP
+        at["words3"] = at["w1b"] + 2 * LAP
+        at["wd_raw"] = at["w1b"] + RAW - LAP
         at["h_bf0"] = at["wd_raw"] + LAP
         at["h_bf1"] = at["h_bf0"] + 1024
-        at["w1b"] = at["wd_raw"] + 8192 - LAP
-        at["words1"] = at["w1b"] + LAP
-        at["words23"] = at["w1b"] + RAW - LAP
-        at["rows"] = at["w1b"] + RAW
-        at["c00"] = at["rows"] + RAW - LAP
-        at["gate"] = at["c00"] + RAW - LAP
-        at["best0"] = at["gate"] + 8192
+        at["best0"] = at["wd_raw"] + 8192
         at["c01"] = at["best0"] + 8192 - LAP
         at["w0a"] = at["c01"] + RAW - LAP
         at["late_rows"] = at["w0a"] + LAP
         at["wc_raw"] = at["w0a"] + RAW - LAP
-        at["w0b"] = at["wc_raw"] + 2048
-        at["picked23"] = at["w0b"] + RAW - LAP
-        at["c10"] = at["picked23"] + 4096
-        at["w1a"] = at["c10"] + RAW - LAP
-        at["c11"] = at["w1a"] + RAW - LAP
-        at["words0"] = at["c11"] + RAW + LAP
+        at["picked2"] = at["wc_raw"] + 2048
+        at["w0b"] = at["picked2"] + 2048 - LAP
+        at["words1"] = at["w0b"] + LAP
+        at["picked3"] = at["w0b"] + RAW - LAP
+        at["words0"] = at["picked3"] + 2048
         at["c_bf1"] = at["words0"] + 2048 - LAP
         at["mid2"] = at["c_bf1"]
         at["mid3"] = at["c_bf1"] + 2048
@@ -122,8 +122,16 @@ def tile_list_pnet_gate_kernel(
 
         cast_w(0, 0)
         cast_w(0, 1)
-        cast_w(1, 0)
-        cast_w(1, 1)
+        c_raw = {(0, 0): load_half(c, 0, 0, "c00")}
+        c_bfs = [tile(f"c_bf{half}", [P, PASSES, HALF * PACK], BF16) for half in range(2)]
+
+        def cast_c(half, a):
+            nc.scalar.copy(
+                c_bfs[half][:, a, :].rearrange("p (x i j) -> p x j i", i=4, j=PACK),
+                c_raw[half, a][:].rearrange("p j (x i) -> p x j i", i=4),
+            )
+
+        cast_c(0, 0)
 
         picked_scales = []
         for s in range(2):
@@ -138,7 +146,8 @@ def tile_list_pnet_gate_kernel(
                 nc.sync.dma_start(planes[32 * q : 32 * q + 4], rows[96 + 8 * q : 96 + 8 * q + 8, :])
 
         move_rows(early_planes, picked_scales[0][:].bitcast(I32))
-        c_raw = {(0, 0): load_half(c, 0, 0, "c00")}
+        cast_w(1, 0)
+        cast_w(1, 1)
         c_raw[0, 1] = load_half(c, 1, 0, "c01")
         wc_raw = tile("wc_raw", [P, PASSES, R // 2], I32)
         nc.sync.dma_start(wc_raw[:], wc_words.rearrange("a p b -> p a b").bitcast(I32))
@@ -172,7 +181,8 @@ def tile_list_pnet_gate_kernel(
         def part_passes(g0, count, name):
             words = tile(name, [P, PASSES, 2 * count * J], U8)
             nc.vector.tensor_copy(
-                words[:].bitcast(U16), picked[g0][:].bitcast(U16).rearrange("p (n d) -> p d n", d=PASSES)
+                words[:].bitcast(U16).rearrange("p d (h n) -> p h d n", h=2),
+                picked[g0][:].bitcast(U16).rearrange("p (h n d) -> p h d n", h=2, d=PASSES),
             )
             for k in range(count):
                 parted[g0 + k] = words[:, :, 2 * k * J : 2 * (k + 1) * J]
@@ -181,10 +191,12 @@ def tile_list_pnet_gate_kernel(
         pick(1, 1, "picked1")
         part_passes(0, 1, "words0")
         quantize_w(0)
-        pick(2, 2, "picked23")
-        quantize_w(1)
+        pick(2, 1, "picked2")
         part_passes(1, 1, "words1")
-        part_passes(2, 2, "words23")
+        pick(3, 1, "picked3")
+        part_passes(2, 1, "words2")
+        quantize_w(1)
+        part_passes(3, 1, "words3")
 
         def project(dst, g, t, a, j0=0, width=J):
             nc.tensor.matmul_mx(
@@ -202,22 +214,12 @@ def tile_list_pnet_gate_kernel(
 
         banks = [new_banks(0), new_banks(1)]
         for a in range(PASSES):
-            for t in range(4):
-                project(banks[0][t][:], 0, t, a)
-        for t in range(4):
-            for a in range(PASSES):
-                project(banks[1][t][:], 1, t, a)
+            for g in range(2):
+                for t in range(4):
+                    project(banks[g][t][:], g, t, a)
 
         c_codes = {}
         c_scales = tile("c_scales", [P, 2, PASSES, HALF], U8)
-
-        def cast_c(dst, half, a):
-            nc.scalar.copy(
-                dst.rearrange("p (x i j) -> p x j i", i=4, j=PACK),
-                c_raw[half, a][:].rearrange("p j (x i) -> p x j i", i=4),
-            )
-
-        c_bfs = [tile(f"c_bf{half}", [P, PASSES, HALF * PACK], BF16) for half in range(2)]
 
         def quantize_c(half):
             c_codes[half] = tile(f"c_codes{half}", [P, PASSES, HALF], U32)
@@ -227,14 +229,13 @@ def tile_list_pnet_gate_kernel(
                 c_bfs[half][:].rearrange("p a x -> p (a x)"),
             )
 
-        for a in range(PASSES):
-            cast_c(c_bfs[0][:, a, :], 0, a)
+        cast_c(0, 1)
         quantize_c(0)
         best = tile("best0", [P, 4, J], F32)
         for t in range(4):
             nc.scalar.copy(best[:, t, :], banks[0][t][:])
         for a in range(PASSES):
-            cast_c(c_bfs[1][:, a, :], 1, a)
+            cast_c(1, a)
 
         wc_codes = tile("wc_codes", [P, PASSES, R // 2], I32)
         nc.vector.tensor_copy(

@@ -23,7 +23,6 @@ K_PASS = P * PACK
 PASSES = K // K_PASS
 HALF = 256
 CHUNK = 128
-CHUNKS = J // CHUNK
 LIST_COLS = J // 16
 
 
@@ -39,39 +38,38 @@ def tile_list_pnet_gate_kernel(
         LAP = 64
         RAW = 4096
         at = {}
-        at["gate"] = 0
-        at["c10"] = at["gate"] + 8192 - LAP
+        at["c10"] = 0
         at["w1a"] = at["c10"] + RAW - LAP
         at["rows"] = at["w1a"] + RAW - LAP
-        at["c11"] = at["rows"]
         at["w1b"] = at["rows"] + RAW - LAP
-        at["words3"] = at["w1b"] + 2 * LAP
-        at["wd_raw"] = at["w1b"] + RAW - LAP
-        at["h_bf0"] = at["wd_raw"] + LAP
-        at["h_bf1"] = at["h_bf0"] + 1024
-        at["best0"] = at["wd_raw"] + 8192
-        at["c01"] = at["best0"] + 8192 - LAP
-        at["w0a"] = at["c01"] + RAW - LAP
-        at["late_rows"] = at["w0a"] + LAP
-        at["wc_raw"] = at["w0a"] + RAW - LAP
-        at["picked2"] = at["wc_raw"] + 2048
-        at["w0b"] = at["picked2"] + 2048 - LAP
-        at["words1"] = at["w0b"] + LAP
-        at["picked3"] = at["w0b"] + RAW - LAP
-        at["words0"] = at["picked3"] + 2048
-        at["c_bf1"] = at["words0"] + 2048 - LAP
-        at["mid2"] = at["c_bf1"]
-        at["mid3"] = at["c_bf1"] + 2048
-        at["pooled0"] = at["c11"] + LAP - 2048
-        at["own_sb0"] = at["c11"] + LAP
-        at["own_sb1"] = at["own_sb0"] + 2048
-        at["wd_codes"] = at["own_sb1"]
-        at["pooled1"] = at["mid3"] + 2048
-        at["mid0"] = at["pooled1"] + 2048 - LAP
-        at["wd_bf0"] = at["mid0"] + LAP
-        at["c_codes0"] = at["wd_bf0"] + 2048
-        at["wd_bf1"] = at["c_codes0"]
-        at["summed3"] = at["wd_bf1"]
+        at["picked3"] = at["w1b"] + LAP
+        at["wc_codes"] = at["picked3"]
+        at["c11"] = at["w1b"] + RAW - LAP
+        at["picked_scales0"] = at["c11"] + 2 * RAW
+        at["c00"] = at["picked_scales0"] + 1024 - LAP
+        at["words3"] = at["c00"] + LAP
+        at["wd_raw"] = at["c00"] + RAW - LAP
+        at["wc_raw"] = at["wd_raw"] + 8192 + 2048
+        at["picked_scales1"] = at["wc_raw"] + 2048 - LAP
+        at["c01"] = at["picked_scales1"] + 1024 - LAP
+        at["gate"] = at["c01"] + RAW - LAP
+        at["w0b"] = at["gate"] + 8192
+        at["late_rows"] = at["w0b"]
+        at["words1"] = at["w0b"] + 1536
+        at["picked2"] = at["w0b"] + RAW - LAP
+        at["first0"] = at["picked2"] + 2048
+        at["c_bf01"] = at["first0"]
+        at["c_bf1"] = at["first0"] + 2048
+        at["first1"] = at["c_bf1"]
+        at["summed0"] = at["c_bf1"]
+        at["summed1"] = at["c_bf1"] + 2048
+        at["own_sb"] = at["c11"] + RAW - LAP
+        at["mid10"] = at["c11"] - LAP
+        at["mid11"] = at["mid10"] + 2048
+        at["mid01"] = at["c01"] + LAP
+        at["pooled0"] = at["mid01"] - RAW
+        at["c_codes0"] = at["c_bf1"] + RAW
+        at["wd_bf"] = at["c_codes0"]
 
         def tile(name, shape, dtype):
             if name in at:
@@ -114,24 +112,22 @@ def tile_list_pnet_gate_kernel(
             if a == 0 and half == 0:
                 nc.scalar.activation(part[:, :, 0], src[:, :, 0], ACT.Copy)
                 nc.scalar.copy(part[:, :, 1:4], src[:, :, 1:4])
-            else:
+            elif half == 0:
                 nc.scalar.copy(part, src)
+            else:
+                for t in (0, 2):
+                    nc.scalar.copy(part[:, :, t : t + 2], src[:, :, t : t + 2])
 
         def quantize_w(a):
-            nc.vector.quantize_mx(w_codes[:, a, :].bitcast(FP8X4), w_scales[:, a, :], w_bfs[a][:])
+            for x in (0, HALF):
+                nc.vector.quantize_mx(
+                    w_codes[:, a, x : x + HALF].bitcast(FP8X4),
+                    w_scales[:, a, x : x + HALF],
+                    w_bfs[a][:, PACK * x : PACK * (x + HALF)],
+                )
 
         cast_w(0, 0)
         cast_w(0, 1)
-        c_raw = {(0, 0): load_half(c, 0, 0, "c00")}
-        c_bfs = [tile(f"c_bf{half}", [P, PASSES, HALF * PACK], BF16) for half in range(2)]
-
-        def cast_c(half, a):
-            nc.scalar.copy(
-                c_bfs[half][:, a, :].rearrange("p (x i j) -> p x j i", i=4, j=PACK),
-                c_raw[half, a][:].rearrange("p j (x i) -> p x j i", i=4),
-            )
-
-        cast_c(0, 0)
 
         picked_scales = []
         for s in range(2):
@@ -148,9 +144,38 @@ def tile_list_pnet_gate_kernel(
         move_rows(early_planes, picked_scales[0][:].bitcast(I32))
         cast_w(1, 0)
         cast_w(1, 1)
-        c_raw[0, 1] = load_half(c, 1, 0, "c01")
-        wc_raw = tile("wc_raw", [P, PASSES, R // 2], I32)
-        nc.sync.dma_start(wc_raw[:], wc_words.rearrange("a p b -> p a b").bitcast(I32))
+
+        def cast_c(dst, a, half):
+            raw = load_half(c, a, half, f"c{half}{a}")
+            nc.scalar.copy(
+                dst.rearrange("p (x i j) -> p x j i", i=4, j=PACK),
+                raw[:].rearrange("p j (x i) -> p x j i", i=4),
+            )
+
+        c_bf00 = tile("c_bf00", [P, HALF * PACK], BF16)
+        cast_c(c_bf00[:], 0, 0)
+
+        parted = {}
+        picked = {}
+
+        def pick(g):
+            picked[g] = tile(f"picked{g}", [P, J], U32)
+            nc.vector.tensor_copy(
+                picked[g][:],
+                table[:].bitcast(U32).indirect(offsets[:, g * LIST_COLS : (g + 1) * LIST_COLS]),
+            )
+
+        def part_passes(g):
+            parted[g] = tile(f"words{g}", [P, PASSES, 2 * J], U8)
+            nc.vector.tensor_copy(
+                parted[g][:].bitcast(U16).rearrange("p d (h n) -> p h d n", h=2),
+                picked[g][:].bitcast(U16).rearrange("p (h n d) -> p h d n", h=2, d=PASSES),
+            )
+
+        pick(0)
+        pick(1)
+        part_passes(0)
+        quantize_w(0)
         late_rows = tile("late_rows", [P, (2 * J + R) // 4], I32)
         nc.vector.tensor_copy(late_rows[96:128, 0 : 2 * J // 4], picked_scales[1][96:128, :].bitcast(I32))
         nc.vector.tensor_copy(
@@ -159,46 +184,26 @@ def tile_list_pnet_gate_kernel(
         )
         move_rows(late_planes, late_rows)
         tab_planes = [early_planes[:].bitcast(U8), late_planes[:].bitcast(U8)]
-        c_raw[1, 0] = load_half(c, 0, 1, "c10")
-        c_raw[1, 1] = load_half(c, 1, 1, "c11")
-        wd_raw = tile("wd_raw", [P, PACK, N], F32)
-        wd_rows = wd.rearrange("(h t i) n -> t h i n", t=4, i=4)
-        for t in range(4):
-            nc.sync.dma_start(wd_raw[:, t, :], wd_rows[t])
-        gate = tile("gate", [P, 4, J], F32)
-        nc.sync.dma_start(gate[:], gm.rearrange("(u p) j -> p u j", p=P))
-
-        parted = {}
-        picked = {}
-
-        def pick(g0, count, name):
-            picked[g0] = tile(name, [P, count * J], U32)
-            nc.vector.tensor_copy(
-                picked[g0][:],
-                table[:].bitcast(U32).indirect(offsets[:, g0 * LIST_COLS : (g0 + count) * LIST_COLS]),
-            )
-
-        def part_passes(g0, count, name):
-            words = tile(name, [P, PASSES, 2 * count * J], U8)
-            nc.vector.tensor_copy(
-                words[:].bitcast(U16).rearrange("p d (h n) -> p h d n", h=2),
-                picked[g0][:].bitcast(U16).rearrange("p (h n d) -> p h d n", h=2, d=PASSES),
-            )
-            for k in range(count):
-                parted[g0 + k] = words[:, :, 2 * k * J : 2 * (k + 1) * J]
-
-        pick(0, 1, "picked0")
-        pick(1, 1, "picked1")
-        part_passes(0, 1, "words0")
-        quantize_w(0)
-        pick(2, 1, "picked2")
-        part_passes(1, 1, "words1")
-        pick(3, 1, "picked3")
-        part_passes(2, 1, "words2")
+        wc_raw = tile("wc_raw", [P, PASSES, R // 2], I32)
+        nc.sync.dma_start(wc_raw[:], wc_words.rearrange("a p b -> p a b").bitcast(I32))
+        pick(2)
+        part_passes(1)
+        part_passes(2)
         quantize_w(1)
-        part_passes(3, 1, "words3")
+        pick(3)
 
-        def project(dst, g, t, a, j0=0, width=J):
+        c_codes = [tile(f"c_codes{half}", [P, PASSES, HALF], U32) for half in range(2)]
+        c_scales = tile("c_scales", [P, 2, PASSES, HALF], U8)
+        nc.vector.quantize_mx(c_codes[0][:, 0, :].bitcast(FP8X4), c_scales[:, 0, 0, :], c_bf00[:])
+        part_passes(3)
+
+        wc_codes = tile("wc_codes", [P, PASSES, R // 2], I32)
+        nc.gpsimd.tensor_copy(
+            wc_codes[:].rearrange("p a (t h x) -> p a t h x", t=4, x=2),
+            wc_raw[:].rearrange("p a (h t x) -> p a t h x", t=4, x=2),
+        )
+
+        def project(dst, g, t, a, j0, width):
             nc.tensor.matmul_mx(
                 out=dst,
                 lhsT=w_codes[:, a, t * P : (t + 1) * P].bitcast(FP8X4),
@@ -209,110 +214,148 @@ def tile_list_pnet_gate_kernel(
                 stop=(a == PASSES - 1),
             )
 
-        def new_banks(g):
-            return [psum.tile([P, J], F32, name=f"a{g}_{t}", tag=f"bank{g % 2}{t}") for t in range(4)]
-
-        banks = [new_banks(0), new_banks(1)]
-        for a in range(PASSES):
+        banks = [[psum.tile([P, J], F32, name=f"a{g}_{t}", tag=f"bank{4 * g + t}") for t in range(4)] for g in range(2)]
+        for g in range(2):
+            for t in range(4):
+                project(banks[g][t][:], g, t, 0, 0, J)
+        for t0 in (0, 2):
             for g in range(2):
-                for t in range(4):
-                    project(banks[g][t][:], g, t, a)
+                for t in (t0, t0 + 1):
+                    project(banks[g][t][:], g, t, 1, 0, J)
 
-        c_codes = {}
-        c_scales = tile("c_scales", [P, 2, PASSES, HALF], U8)
-
-        def quantize_c(half):
-            c_codes[half] = tile(f"c_codes{half}", [P, PASSES, HALF], U32)
-            nc.vector.quantize_mx(
-                c_codes[half][:].rearrange("p a x -> p (a x)").bitcast(FP8X4),
-                c_scales[:, half].rearrange("p a x -> p (a x)"),
-                c_bfs[half][:].rearrange("p a x -> p (a x)"),
-            )
-
-        cast_c(0, 1)
-        quantize_c(0)
-        best = tile("best0", [P, 4, J], F32)
+        first = [tile(f"first{t}", [P, J], F32) for t in range(4)]
+        best = tile("best", [P, 4, J], F32)
         for t in range(4):
-            nc.scalar.copy(best[:, t, :], banks[0][t][:])
+            nc.scalar.copy(first[t][:], banks[0][t][:])
+        for t in range(4):
+            nc.vector.tensor_tensor(best[:, t, :], banks[1][t][:], first[t][:], ALU.max)
+
+        c_bf01 = tile("c_bf01", [P, HALF * PACK], BF16)
+        cast_c(c_bf01[:], 1, 0)
+        c_bf1 = tile("c_bf1", [P, PASSES, HALF * PACK], BF16)
         for a in range(PASSES):
-            cast_c(1, a)
-
-        wc_codes = tile("wc_codes", [P, PASSES, R // 2], I32)
-        nc.vector.tensor_copy(
-            wc_codes[:].rearrange("p a (t h x) -> p a t h x", t=4, x=2),
-            wc_raw[:].rearrange("p a (h t x) -> p a t h x", t=4, x=2),
-        )
-        best1 = tile("best1", [P, 4, J], F32)
+            cast_c(c_bf1[:, a, :], a, 1)
+        wd_raw = tile("wd_raw", [P, PACK, N], F32)
+        wd_rows = wd.rearrange("(h t i) n -> t h i n", t=4, i=4)
         for t in range(4):
-            nc.vector.tensor_tensor(best1[:, t, :], banks[1][t][:], best[:, t, :], ALU.max)
+            nc.sync.dma_start(wd_raw[:, t, :], wd_rows[t])
+        gate = tile("gate", [P, 4, J], F32)
+        nc.sync.dma_start(gate[:], gm.rearrange("(u p) j -> p u j", p=P))
 
         late = {}
 
-        def project_late(g, ch, tag):
-            bank = psum.tile([P, 4, CHUNK], F32, name=f"a{g}_{ch}", tag=tag)
-            for t in range(4):
+        def project_late(g, half, pair, tag):
+            bank = psum.tile([P, 2, HALF], F32, name=f"a{g}_{half}{pair}", tag=tag)
+            for k in range(2):
                 for a in range(PASSES):
-                    project(bank[:, t, :], g, t, a, ch * CHUNK, CHUNK)
-            late[g, ch] = bank
+                    project(bank[:, k, :], g, 2 * pair + k, a, half * HALF, HALF)
+            late[g, half, pair] = bank
 
         wc_bytes = wc_codes[:].bitcast(U8)
         wc_scale_bytes = tab_planes[1][:, :, 2 * J :]
-        out_rows = out.rearrange("(u p) j -> p u j", p=P)
-        own, pooled, h_bf, ys = {}, {}, {}, {}
 
-        def project_own(ch, tag):
-            half, x0 = divmod(ch * CHUNK, HALF)
-            own[ch] = psum.tile([P, 4, CHUNK], F32, name=f"own{ch}", tag=tag)
-            for t in range(4):
-                for a in range(PASSES):
-                    nc.tensor.matmul_mx(
-                        out=own[ch][:, t, :],
-                        lhsT=wc_bytes[:, a, 2 * t * P : 2 * (t + 1) * P].bitcast(FP4X4),
-                        lhsT_scale=wc_scale_bytes[:, a, t * P : (t + 1) * P],
-                        rhs=c_codes[half][:, a, x0 : x0 + CHUNK].bitcast(FP8X4),
-                        rhs_scale=c_scales[:, half, a, x0 : x0 + CHUNK],
-                        start=(a == 0),
-                        stop=(a == PASSES - 1),
-                    )
+        def project_own(dst, t, half, x0, width):
+            for a in range(PASSES):
+                nc.tensor.matmul_mx(
+                    out=dst,
+                    lhsT=wc_bytes[:, a, 2 * t * P : 2 * (t + 1) * P].bitcast(FP4X4),
+                    lhsT_scale=wc_scale_bytes[:, a, t * P : (t + 1) * P],
+                    rhs=c_codes[half][:, a, x0 : x0 + width].bitcast(FP8X4),
+                    rhs_scale=c_scales[:, half, a, x0 : x0 + width],
+                    start=(a == 0),
+                    stop=(a == PASSES - 1),
+                )
 
-        mid, own_sb = {}, {}
+        mid = {}
+        pooled = [tile(f"pooled{half}", [P, 4, HALF], F32) for half in range(2)]
 
-        def pool_mid(ch):
-            mid[ch] = tile(f"mid{ch}", [P, 4, CHUNK], F32)
+        def pool_mid(half, pair):
+            cols = slice(half * HALF, (half + 1) * HALF)
+            mid[half, pair] = tile(f"mid{half}{pair}", [P, 2, HALF], F32)
             nc.vector.tensor_tensor(
-                mid[ch][:], late[2, ch][:], best1[:, :, ch * CHUNK : (ch + 1) * CHUNK], ALU.max
+                mid[half, pair][:], late[2, half, pair][:], best[:, 2 * pair : 2 * pair + 2, cols], ALU.max
             )
 
-        def pool_last(ch):
-            pooled[ch] = tile(f"pooled{ch}", [P, 4, CHUNK], F32)
-            nc.vector.tensor_tensor(pooled[ch][:], late[3, ch][:], mid[ch][:], ALU.max)
+        def pool_last(half, pair):
+            nc.vector.tensor_tensor(
+                pooled[half][:, 2 * pair : 2 * pair + 2, :], late[3, half, pair][:], mid[half, pair][:], ALU.max
+            )
 
-        def copy_own(ch):
-            own_sb[ch] = tile(f"own_sb{ch}", [P, 4, CHUNK], F32)
-            nc.scalar.copy(own_sb[ch][:], own[ch][:])
+        for g in (2, 3):
+            for pair in range(2):
+                project_late(g, 0, pair, f"bank{2 * (g - 2) + pair}")
+        project_late(2, 1, 0, "bank6")
+        pool_mid(0, 0)
+        nc.vector.quantize_mx(c_codes[0][:, 1, :].bitcast(FP8X4), c_scales[:, 0, 1, :], c_bf01[:])
+        pool_mid(0, 1)
+        own_sb = tile("own_sb", [P, 4, HALF], F32)
+        for pair in range(2):
+            own = psum.tile([P, 2, HALF], F32, name=f"own0{pair}", tag=f"bank{4 + pair}")
+            for k in range(2):
+                project_own(own[:, k, :], 2 * pair + k, 0, 0, HALF)
+            nc.scalar.copy(own_sb[:, 2 * pair : 2 * pair + 2, :], own[:])
+        project_late(2, 1, 1, "bank1")
+        for pair in range(2):
+            pool_last(0, pair)
+        nc.vector.quantize_mx(
+            c_codes[1][:].rearrange("p a x -> p (a x)").bitcast(FP8X4),
+            c_scales[:, 1].rearrange("p a x -> p (a x)"),
+            c_bf1[:].rearrange("p a x -> p (a x)"),
+        )
+        for pair in range(2):
+            project_late(3, 1, pair, f"bank{2 + pair}")
+        owns = {}
+        for ch in range(2):
+            owns[ch] = psum.tile([P, 4, CHUNK], F32, name=f"own1{ch}", tag=("bank7", "bank0")[ch])
+            for t in range(4):
+                project_own(owns[ch][:, t, :], t, 1, ch * CHUNK, CHUNK)
+        summed = {}
+        for ch in range(2):
+            cols = slice(ch * CHUNK, (ch + 1) * CHUNK)
+            summed[ch] = tile(f"summed{ch}", [P, 4, CHUNK], F32)
+            nc.gpsimd.tensor_tensor(summed[ch][:], own_sb[:, :, cols], pooled[0][:, :, cols], ALU.add)
+        for pair in range(2):
+            pool_mid(1, pair)
+        for pair in range(2):
+            pool_last(1, pair)
 
-        def add_own(ch):
-            summed = tile(f"summed{ch}", [P, 4, CHUNK], F32)
-            if ch < 2:
-                nc.gpsimd.tensor_tensor(summed[:], own_sb[ch][:], pooled[ch][:], ALU.add)
-            else:
-                nc.vector.tensor_tensor(summed[:], own[ch][:], pooled[ch][:], ALU.add)
+        wd_bf = tile("wd_bf", [P, N * PACK], BF16)
+        for half in range(2):
+            nc.scalar.copy(
+                wd_bf[:, half * HALF * PACK : (half + 1) * HALF * PACK].rearrange("p (x i t) -> p x t i", i=4, t=PACK),
+                wd_raw[:, :, half * HALF : (half + 1) * HALF].rearrange("p t (x i) -> p x t i", i=4),
+            )
+
+        for ch in range(2):
+            cols = slice(ch * CHUNK, (ch + 1) * CHUNK)
+            summed[2 + ch] = tile(f"summed{2 + ch}", [P, 4, CHUNK], F32)
+            nc.vector.tensor_tensor(summed[2 + ch][:], owns[ch][:], pooled[1][:, :, cols], ALU.add)
+        h_bf = {}
+        for ch in range(4):
             h_bf[ch] = tile(f"h_bf{ch}", [P, CHUNK * PACK], BF16)
             nc.scalar.activation(
                 h_bf[ch][:].rearrange("p (x i t) -> p x t i", i=4, t=PACK),
-                summed[:].rearrange("p t (x i) -> p x t i", i=4),
+                summed[ch][:].rearrange("p t (x i) -> p x t i", i=4),
                 ACT.Relu,
             )
 
+        wd_codes = tile("wd_codes", [P, N], U32)
+        wd_scales = tile("wd_scales", [P, N], U8)
+        nc.vector.quantize_mx(wd_codes[:].bitcast(FP8X4), wd_scales[:], wd_bf[:])
+
+        out_rows = out.rearrange("(u p) j -> p u j", p=P)
+
+        ys = {}
+
         def second_layer(ch):
-            h_codes = keep.tile([P, CHUNK], U32, name=f"h_codes{ch}", align_bytes=64)
-            h_scales = keep.tile([P, CHUNK], U8, name=f"h_scales{ch}", align_bytes=64)
+            h_codes = tile(f"h_codes{ch}", [P, CHUNK], U32)
+            h_scales = tile(f"h_scales{ch}", [P, CHUNK], U8)
             nc.vector.quantize_mx(h_codes[:].bitcast(FP8X4), h_scales[:], h_bf[ch][:])
-            ys[ch] = psum.tile([P, 4, CHUNK], F32, name=f"y{ch}", tag=f"bank1{ch}")
+            ys[ch] = psum.tile([P, 4, CHUNK], F32, name=f"y{ch}", tag=("bank4", "bank5", "bank6", "bank1")[ch])
             for u in range(4):
                 nc.tensor.matmul_mx(
                     out=ys[ch][:, u, :],
-                    lhsT=wd_q[0][:, u * P : (u + 1) * P].bitcast(FP8X4),
+                    lhsT=wd_codes[:, u * P : (u + 1) * P].bitcast(FP8X4),
                     lhsT_scale=wd_scales[:, u * P : (u + 1) * P],
                     rhs=h_codes[:].bitcast(FP8X4),
                     rhs_scale=h_scales[:],
@@ -322,57 +365,14 @@ def tile_list_pnet_gate_kernel(
 
         def finish(ch):
             cols = slice(ch * CHUNK, (ch + 1) * CHUNK)
-            res = keep.tile([P, 4, CHUNK], F32, name=f"res{ch}")
-            step = 2 if ch == CHUNKS - 1 else 4
+            res = tile(f"res{ch}", [P, 4, CHUNK], F32)
+            step = 2 if ch == 3 else 4
             for u in range(0, 4, step):
                 us = slice(u, u + step)
                 nc.vector.tensor_tensor(res[:, us, :], ys[ch][:, us, :], gate[:, us, cols], ALU.mult)
                 nc.sync.dma_start(out_rows[:, us, cols], res[:, us, :])
 
-        project_late(2, 0, "bank00")
-        project_late(2, 1, "bank01")
-        project_late(3, 0, "bank02")
-        project_own(0, "bank03")
-        copy_own(0)
-        project_late(2, 2, "bank10")
-        project_late(3, 1, "bank11")
-        project_own(1, "bank12")
-        copy_own(1)
-        project_late(2, 3, "bank13")
-        wd_bf = {}
-
-        def cast_wd(half):
-            wd_bf[half] = tile(f"wd_bf{half}", [P, HALF * PACK], BF16)
-            nc.scalar.copy(
-                wd_bf[half][:].rearrange("p (x i t) -> p x t i", i=4, t=PACK),
-                wd_raw[:, :, half * HALF : (half + 1) * HALF].rearrange("p t (x i) -> p x t i", i=4),
-            )
-
-        pool_mid(0)
-        project_late(3, 2, "bank00")
-        pool_mid(1)
-        project_late(3, 3, "bank01")
-        quantize_c(1)
-        pool_last(0)
-        project_own(2, "bank02")
-        project_own(3, "bank03")
-        cast_wd(0)
-        cast_wd(1)
-        add_own(0)
-        pool_mid(2)
-        pool_last(1)
-        add_own(1)
-        pool_mid(3)
-        pool_last(2)
-        pool_last(3)
-        add_own(2)
-        wd_q = [tile("wd_codes", [P, N], U32)]
-        wd_scales = tile("wd_scales", [P, N], U8)
-        for half in range(2):
-            cols = slice(half * HALF, (half + 1) * HALF)
-            nc.vector.quantize_mx(wd_q[0][:, cols].bitcast(FP8X4), wd_scales[:, cols], wd_bf[half][:])
         second_layer(0)
-        add_own(3)
         second_layer(1)
         finish(0)
         second_layer(2)

@@ -38,38 +38,39 @@ def tile_list_pnet_gate_kernel(
         LAP = 64
         RAW = 4096
         at = {}
-        at["c10"] = 0
-        at["w1a"] = at["c10"] + RAW - LAP
-        at["rows"] = at["w1a"] + RAW - LAP
+        at["gate"] = 0
+        at["c00"] = at["gate"] + 8192 - LAP
+        at["rows"] = at["c00"] + RAW - LAP
         at["w1b"] = at["rows"] + RAW - LAP
         at["picked3"] = at["w1b"] + LAP
         at["wc_codes"] = at["picked3"]
-        at["c11"] = at["w1b"] + RAW - LAP
-        at["picked_scales0"] = at["c11"] + 2 * RAW
-        at["c00"] = at["picked_scales0"] + 1024 - LAP
-        at["words3"] = at["c00"] + LAP
-        at["wd_raw"] = at["c00"] + RAW - LAP
-        at["wc_raw"] = at["wd_raw"] + 8192 + 2048
+        at["wd_raw"] = at["w1b"] + RAW - LAP
+        at["w0a"] = at["wd_raw"] + 8192
+        at["c01"] = at["w0a"] + RAW - LAP
+        at["words3"] = at["c01"] + LAP
+        at["first"] = at["c01"] + RAW - LAP
+        at["wc_raw"] = at["first"] + 8192 + 2048
         at["picked_scales1"] = at["wc_raw"] + 2048 - LAP
-        at["c01"] = at["picked_scales1"] + 1024 - LAP
-        at["gate"] = at["c01"] + RAW - LAP
-        at["w0b"] = at["gate"] + 8192
+        at["c10"] = at["picked_scales1"] + 1024 - LAP
+        at["wd_bf"] = at["c10"] + LAP - RAW
+        at["own_sb"] = at["c10"] + LAP
+        at["h_bf2"] = at["own_sb"]
+        at["h_bf3"] = at["own_sb"] + 1024
+        at["w1a"] = at["own_sb"] + RAW
+        at["c11"] = at["w1a"] + RAW - LAP
+        at["mid10"] = at["c11"]
+        at["mid11"] = at["mid10"] + 2048
+        at["wd_codes"] = at["mid10"] + LAP - 2048
+        at["summed2"] = at["wd_raw"] + LAP
+        at["w0b"] = at["c11"] + RAW
         at["late_rows"] = at["w0b"]
         at["words1"] = at["w0b"] + 1536
         at["picked2"] = at["w0b"] + RAW - LAP
-        at["first0"] = at["picked2"] + 2048
-        at["c_bf01"] = at["first0"]
-        at["c_bf1"] = at["first0"] + 2048
-        at["first1"] = at["c_bf1"]
+        at["c_bf1"] = at["picked2"] + 2048
+        at["c_bf0"] = at["c_bf1"]
         at["summed0"] = at["c_bf1"]
         at["summed1"] = at["c_bf1"] + 2048
-        at["own_sb"] = at["c11"] + RAW - LAP
-        at["mid10"] = at["c11"] - LAP
-        at["mid11"] = at["mid10"] + 2048
-        at["mid01"] = at["c01"] + LAP
-        at["pooled0"] = at["mid01"] - RAW
-        at["c_codes0"] = at["c_bf1"] + RAW
-        at["wd_bf"] = at["c_codes0"]
+        at["summed3"] = at["summed0"]
 
         def tile(name, shape, dtype):
             if name in at:
@@ -152,8 +153,9 @@ def tile_list_pnet_gate_kernel(
                 raw[:].rearrange("p j (x i) -> p x j i", i=4),
             )
 
-        c_bf00 = tile("c_bf00", [P, HALF * PACK], BF16)
-        cast_c(c_bf00[:], 0, 0)
+        c_bf0 = tile("c_bf0", [P, PASSES, HALF * PACK], BF16)
+        for a in range(PASSES):
+            cast_c(c_bf0[:, a, :], a, 0)
 
         parted = {}
         picked = {}
@@ -194,7 +196,15 @@ def tile_list_pnet_gate_kernel(
 
         c_codes = [tile(f"c_codes{half}", [P, PASSES, HALF], U32) for half in range(2)]
         c_scales = tile("c_scales", [P, 2, PASSES, HALF], U8)
-        nc.vector.quantize_mx(c_codes[0][:, 0, :].bitcast(FP8X4), c_scales[:, 0, 0, :], c_bf00[:])
+
+        def quantize_c(half, c_bf):
+            nc.vector.quantize_mx(
+                c_codes[half][:].rearrange("p a x -> p (a x)").bitcast(FP8X4),
+                c_scales[:, half].rearrange("p a x -> p (a x)"),
+                c_bf[:].rearrange("p a x -> p (a x)"),
+            )
+
+        quantize_c(0, c_bf0)
         part_passes(3)
 
         wc_codes = tile("wc_codes", [P, PASSES, R // 2], I32)
@@ -223,15 +233,13 @@ def tile_list_pnet_gate_kernel(
                 for t in (t0, t0 + 1):
                     project(banks[g][t][:], g, t, 1, 0, J)
 
-        first = [tile(f"first{t}", [P, J], F32) for t in range(4)]
+        first = tile("first", [P, 4, J], F32)
         best = tile("best", [P, 4, J], F32)
         for t in range(4):
-            nc.scalar.copy(first[t][:], banks[0][t][:])
+            nc.scalar.copy(first[:, t, :], banks[0][t][:])
         for t in range(4):
-            nc.vector.tensor_tensor(best[:, t, :], banks[1][t][:], first[t][:], ALU.max)
+            nc.vector.tensor_tensor(best[:, t, :], banks[1][t][:], first[:, t, :], ALU.max)
 
-        c_bf01 = tile("c_bf01", [P, HALF * PACK], BF16)
-        cast_c(c_bf01[:], 1, 0)
         c_bf1 = tile("c_bf1", [P, PASSES, HALF * PACK], BF16)
         for a in range(PASSES):
             cast_c(c_bf1[:, a, :], a, 1)
@@ -267,7 +275,7 @@ def tile_list_pnet_gate_kernel(
                 )
 
         mid = {}
-        pooled = [tile(f"pooled{half}", [P, 4, HALF], F32) for half in range(2)]
+        pooled = [tile(f"pooled{half}", [P, 2, 4, CHUNK], F32) for half in range(2)]
 
         def pool_mid(half, pair):
             cols = slice(half * HALF, (half + 1) * HALF)
@@ -278,42 +286,39 @@ def tile_list_pnet_gate_kernel(
 
         def pool_last(half, pair):
             nc.vector.tensor_tensor(
-                pooled[half][:, 2 * pair : 2 * pair + 2, :], late[3, half, pair][:], mid[half, pair][:], ALU.max
+                pooled[half][:, :, 2 * pair : 2 * pair + 2, :],
+                late[3, half, pair][:].rearrange("p t (c x) -> p c t x", c=2),
+                mid[half, pair][:].rearrange("p t (c x) -> p c t x", c=2),
+                ALU.max,
             )
 
         for g in (2, 3):
             for pair in range(2):
                 project_late(g, 0, pair, f"bank{2 * (g - 2) + pair}")
-        project_late(2, 1, 0, "bank6")
         pool_mid(0, 0)
-        nc.vector.quantize_mx(c_codes[0][:, 1, :].bitcast(FP8X4), c_scales[:, 0, 1, :], c_bf01[:])
         pool_mid(0, 1)
-        own_sb = tile("own_sb", [P, 4, HALF], F32)
+        own_sb = tile("own_sb", [P, 2, 4, CHUNK], F32)
         for pair in range(2):
             own = psum.tile([P, 2, HALF], F32, name=f"own0{pair}", tag=f"bank{4 + pair}")
             for k in range(2):
                 project_own(own[:, k, :], 2 * pair + k, 0, 0, HALF)
-            nc.scalar.copy(own_sb[:, 2 * pair : 2 * pair + 2, :], own[:])
-        project_late(2, 1, 1, "bank1")
+            nc.scalar.copy(own_sb[:, :, 2 * pair : 2 * pair + 2, :], own[:].rearrange("p t (c x) -> p c t x", c=2))
+        for pair in range(2):
+            project_late(2, 1, pair, f"bank{pair}")
         for pair in range(2):
             pool_last(0, pair)
-        nc.vector.quantize_mx(
-            c_codes[1][:].rearrange("p a x -> p (a x)").bitcast(FP8X4),
-            c_scales[:, 1].rearrange("p a x -> p (a x)"),
-            c_bf1[:].rearrange("p a x -> p (a x)"),
-        )
+        quantize_c(1, c_bf1)
         for pair in range(2):
             project_late(3, 1, pair, f"bank{2 + pair}")
         owns = {}
         for ch in range(2):
-            owns[ch] = psum.tile([P, 4, CHUNK], F32, name=f"own1{ch}", tag=("bank7", "bank0")[ch])
+            owns[ch] = psum.tile([P, 4, CHUNK], F32, name=f"own1{ch}", tag=f"bank{6 + ch}")
             for t in range(4):
                 project_own(owns[ch][:, t, :], t, 1, ch * CHUNK, CHUNK)
         summed = {}
         for ch in range(2):
-            cols = slice(ch * CHUNK, (ch + 1) * CHUNK)
             summed[ch] = tile(f"summed{ch}", [P, 4, CHUNK], F32)
-            nc.gpsimd.tensor_tensor(summed[ch][:], own_sb[:, :, cols], pooled[0][:, :, cols], ALU.add)
+            nc.gpsimd.tensor_tensor(summed[ch][:], own_sb[:, ch], pooled[0][:, ch], ALU.add)
         for pair in range(2):
             pool_mid(1, pair)
         for pair in range(2):
@@ -326,12 +331,13 @@ def tile_list_pnet_gate_kernel(
                 wd_raw[:, :, half * HALF : (half + 1) * HALF].rearrange("p t (x i) -> p x t i", i=4),
             )
 
-        for ch in range(2):
-            cols = slice(ch * CHUNK, (ch + 1) * CHUNK)
-            summed[2 + ch] = tile(f"summed{2 + ch}", [P, 4, CHUNK], F32)
-            nc.vector.tensor_tensor(summed[2 + ch][:], owns[ch][:], pooled[1][:, :, cols], ALU.add)
+        def add_late(ch):
+            summed[ch] = tile(f"summed{ch}", [P, 4, CHUNK], F32)
+            nc.vector.tensor_tensor(summed[ch][:], owns[ch - 2][:], pooled[1][:, ch - 2], ALU.add)
+
         h_bf = {}
-        for ch in range(4):
+
+        def relu(ch):
             h_bf[ch] = tile(f"h_bf{ch}", [P, CHUNK * PACK], BF16)
             nc.scalar.activation(
                 h_bf[ch][:].rearrange("p (x i t) -> p x t i", i=4, t=PACK),
@@ -339,6 +345,8 @@ def tile_list_pnet_gate_kernel(
                 ACT.Relu,
             )
 
+        relu(0)
+        relu(1)
         wd_codes = tile("wd_codes", [P, N], U32)
         wd_scales = tile("wd_scales", [P, N], U8)
         nc.vector.quantize_mx(wd_codes[:].bitcast(FP8X4), wd_scales[:], wd_bf[:])
@@ -351,7 +359,7 @@ def tile_list_pnet_gate_kernel(
             h_codes = tile(f"h_codes{ch}", [P, CHUNK], U32)
             h_scales = tile(f"h_scales{ch}", [P, CHUNK], U8)
             nc.vector.quantize_mx(h_codes[:].bitcast(FP8X4), h_scales[:], h_bf[ch][:])
-            ys[ch] = psum.tile([P, 4, CHUNK], F32, name=f"y{ch}", tag=("bank4", "bank5", "bank6", "bank1")[ch])
+            ys[ch] = psum.tile([P, 4, CHUNK], F32, name=f"y{ch}", tag=f"bank{(4 + ch) % 6}")
             for u in range(4):
                 nc.tensor.matmul_mx(
                     out=ys[ch][:, u, :],
@@ -372,7 +380,11 @@ def tile_list_pnet_gate_kernel(
                 nc.vector.tensor_tensor(res[:, us, :], ys[ch][:, us, :], gate[:, us, cols], ALU.mult)
                 nc.sync.dma_start(out_rows[:, us, cols], res[:, us, :])
 
+        add_late(2)
+        relu(2)
         second_layer(0)
+        add_late(3)
+        relu(3)
         second_layer(1)
         finish(0)
         second_layer(2)

@@ -42,35 +42,34 @@ def tile_list_pnet_gate_kernel(
         at["c00"] = at["gate"] + 8192 - LAP
         at["rows"] = at["c00"] + RAW - LAP
         at["w1b"] = at["rows"] + RAW - LAP
-        at["picked3"] = at["w1b"] + LAP
-        at["wc_codes"] = at["picked3"]
-        at["wd_raw"] = at["w1b"] + RAW - LAP
-        at["w0a"] = at["wd_raw"] + 8192
+        at["picked3"] = at["w1b"] + RAW - LAP
+        at["wc_codes"] = at["picked3"] + LAP
+        at["c_bf0"] = at["picked3"] + 2048
+        at["c_bf1"] = at["c_bf0"] + LAP
+        at["summed1"] = at["c_bf1"]
+        at["summed3"] = at["summed1"]
+        at["w0a"] = at["c_bf1"] + RAW
         at["c01"] = at["w0a"] + RAW - LAP
-        at["words3"] = at["c01"] + LAP
         at["first"] = at["c01"] + RAW - LAP
         at["wc_raw"] = at["first"] + 8192 + 2048
         at["picked_scales1"] = at["wc_raw"] + 2048 - LAP
         at["c10"] = at["picked_scales1"] + 1024 - LAP
         at["wd_bf"] = at["c10"] + LAP - RAW
+        at["summed2"] = at["wd_bf"]
         at["own_sb"] = at["c10"] + LAP
         at["h_bf2"] = at["own_sb"]
-        at["h_bf3"] = at["own_sb"] + 1024
-        at["w1a"] = at["own_sb"] + RAW
+        at["h_codes0"] = at["h_bf2"] + 1024
+        at["wd_codes"] = at["own_sb"] + 2048 - LAP
+        at["wd_raw"] = at["wd_codes"] + 2048
+        at["w1a"] = at["wd_raw"] + 8192 - LAP
         at["c11"] = at["w1a"] + RAW - LAP
-        at["mid10"] = at["c11"]
+        at["summed0"] = at["c11"] + LAP - 2048
+        at["mid10"] = at["c11"] + LAP
         at["mid11"] = at["mid10"] + 2048
-        at["wd_codes"] = at["mid10"] + LAP - 2048
-        at["summed2"] = at["wd_raw"] + LAP
-        at["w0b"] = at["c11"] + RAW
+        at["w0b"] = at["mid11"] + 2048
         at["late_rows"] = at["w0b"]
         at["words1"] = at["w0b"] + 1536
         at["picked2"] = at["w0b"] + RAW - LAP
-        at["c_bf1"] = at["picked2"] + 2048
-        at["c_bf0"] = at["c_bf1"]
-        at["summed0"] = at["c_bf1"]
-        at["summed1"] = at["c_bf1"] + 2048
-        at["summed3"] = at["summed0"]
 
         def tile(name, shape, dtype):
             if name in at:
@@ -89,6 +88,7 @@ def tile_list_pnet_gate_kernel(
 
         wcs_rows = tile("wcs_rows", [P, R // 4], I32)
         nc.sync.dma_start(wcs_rows[96:128, :], wc_scales.rearrange("a q n -> q a n").bitcast(I32))
+        nc.vector.memset(wcs_rows[0:96, :], 0)
 
         early_planes = tile("early_planes", [P, PASSES, 2 * J // 4], I32)
         nc.gpsimd.memset(early_planes[:], 0)
@@ -179,10 +179,10 @@ def tile_list_pnet_gate_kernel(
         part_passes(0)
         quantize_w(0)
         late_rows = tile("late_rows", [P, (2 * J + R) // 4], I32)
-        nc.vector.tensor_copy(late_rows[96:128, 0 : 2 * J // 4], picked_scales[1][96:128, :].bitcast(I32))
+        nc.vector.tensor_copy(late_rows[:, 0 : 2 * J // 4], picked_scales[1][:].bitcast(I32))
         nc.vector.tensor_copy(
-            late_rows[96:128, 2 * J // 4 :].rearrange("p (t h) -> p t h", t=4),
-            wcs_rows[96:128, :].rearrange("p (h t) -> p t h", t=4),
+            late_rows[:, 2 * J // 4 :].rearrange("p (t h) -> p t h", t=4),
+            wcs_rows[:].rearrange("p (h t) -> p t h", t=4),
         )
         move_rows(late_planes, late_rows)
         tab_planes = [early_planes[:].bitcast(U8), late_planes[:].bitcast(U8)]
@@ -193,6 +193,7 @@ def tile_list_pnet_gate_kernel(
         part_passes(2)
         quantize_w(1)
         pick(3)
+        part_passes(3)
 
         c_codes = [tile(f"c_codes{half}", [P, PASSES, HALF], U32) for half in range(2)]
         c_scales = tile("c_scales", [P, 2, PASSES, HALF], U8)
@@ -205,7 +206,6 @@ def tile_list_pnet_gate_kernel(
             )
 
         quantize_c(0, c_bf0)
-        part_passes(3)
 
         wc_codes = tile("wc_codes", [P, PASSES, R // 2], I32)
         nc.gpsimd.tensor_copy(
@@ -262,17 +262,22 @@ def tile_list_pnet_gate_kernel(
         wc_bytes = wc_codes[:].bitcast(U8)
         wc_scale_bytes = tab_planes[1][:, :, 2 * J :]
 
-        def project_own(dst, t, half, x0, width):
-            for a in range(PASSES):
-                nc.tensor.matmul_mx(
-                    out=dst,
-                    lhsT=wc_bytes[:, a, 2 * t * P : 2 * (t + 1) * P].bitcast(FP4X4),
-                    lhsT_scale=wc_scale_bytes[:, a, t * P : (t + 1) * P],
-                    rhs=c_codes[half][:, a, x0 : x0 + width].bitcast(FP8X4),
-                    rhs_scale=c_scales[:, half, a, x0 : x0 + width],
-                    start=(a == 0),
-                    stop=(a == PASSES - 1),
-                )
+        owns = {}
+
+        def project_own(ch, tag):
+            half, x0 = divmod(ch * CHUNK, HALF)
+            owns[ch] = psum.tile([P, 4, CHUNK], F32, name=f"own{ch}", tag=tag)
+            for t in range(4):
+                for a in range(PASSES):
+                    nc.tensor.matmul_mx(
+                        out=owns[ch][:, t, :],
+                        lhsT=wc_bytes[:, a, 2 * t * P : 2 * (t + 1) * P].bitcast(FP4X4),
+                        lhsT_scale=wc_scale_bytes[:, a, t * P : (t + 1) * P],
+                        rhs=c_codes[half][:, a, x0 : x0 + CHUNK].bitcast(FP8X4),
+                        rhs_scale=c_scales[:, half, a, x0 : x0 + CHUNK],
+                        start=(a == 0),
+                        stop=(a == PASSES - 1),
+                    )
 
         mid = {}
         pooled = [tile(f"pooled{half}", [P, 2, 4, CHUNK], F32) for half in range(2)]
@@ -297,12 +302,10 @@ def tile_list_pnet_gate_kernel(
                 project_late(g, 0, pair, f"bank{2 * (g - 2) + pair}")
         pool_mid(0, 0)
         pool_mid(0, 1)
-        own_sb = tile("own_sb", [P, 2, 4, CHUNK], F32)
-        for pair in range(2):
-            own = psum.tile([P, 2, HALF], F32, name=f"own0{pair}", tag=f"bank{4 + pair}")
-            for k in range(2):
-                project_own(own[:, k, :], 2 * pair + k, 0, 0, HALF)
-            nc.scalar.copy(own_sb[:, :, 2 * pair : 2 * pair + 2, :], own[:].rearrange("p t (c x) -> p c t x", c=2))
+        project_own(1, "bank4")
+        project_own(0, "bank5")
+        own_sb = tile("own_sb", [P, 4, CHUNK], F32)
+        nc.scalar.copy(own_sb[:], owns[1][:])
         for pair in range(2):
             project_late(2, 1, pair, f"bank{pair}")
         for pair in range(2):
@@ -310,15 +313,16 @@ def tile_list_pnet_gate_kernel(
         quantize_c(1, c_bf1)
         for pair in range(2):
             project_late(3, 1, pair, f"bank{2 + pair}")
-        owns = {}
-        for ch in range(2):
-            owns[ch] = psum.tile([P, 4, CHUNK], F32, name=f"own1{ch}", tag=f"bank{6 + ch}")
-            for t in range(4):
-                project_own(owns[ch][:, t, :], t, 1, ch * CHUNK, CHUNK)
-        summed = {}
-        for ch in range(2):
+        project_own(2, "bank6")
+        project_own(3, "bank7")
+        summed = {1: tile("summed1", [P, 4, CHUNK], F32)}
+        nc.gpsimd.tensor_tensor(summed[1][:], own_sb[:], pooled[0][:, 1], ALU.add)
+
+        def add_own(ch):
             summed[ch] = tile(f"summed{ch}", [P, 4, CHUNK], F32)
-            nc.gpsimd.tensor_tensor(summed[ch][:], own_sb[:, ch], pooled[0][:, ch], ALU.add)
+            nc.vector.tensor_tensor(summed[ch][:], owns[ch][:], pooled[ch // 2][:, ch % 2], ALU.add)
+
+        add_own(0)
         for pair in range(2):
             pool_mid(1, pair)
         for pair in range(2):
@@ -330,10 +334,6 @@ def tile_list_pnet_gate_kernel(
                 wd_bf[:, half * HALF * PACK : (half + 1) * HALF * PACK].rearrange("p (x i t) -> p x t i", i=4, t=PACK),
                 wd_raw[:, :, half * HALF : (half + 1) * HALF].rearrange("p t (x i) -> p x t i", i=4),
             )
-
-        def add_late(ch):
-            summed[ch] = tile(f"summed{ch}", [P, 4, CHUNK], F32)
-            nc.vector.tensor_tensor(summed[ch][:], owns[ch - 2][:], pooled[1][:, ch - 2], ALU.add)
 
         h_bf = {}
 
@@ -380,12 +380,12 @@ def tile_list_pnet_gate_kernel(
                 nc.vector.tensor_tensor(res[:, us, :], ys[ch][:, us, :], gate[:, us, cols], ALU.mult)
                 nc.sync.dma_start(out_rows[:, us, cols], res[:, us, :])
 
-        add_late(2)
-        relu(2)
         second_layer(0)
-        add_late(3)
-        relu(3)
+        add_own(2)
+        relu(2)
         second_layer(1)
+        add_own(3)
+        relu(3)
         finish(0)
         second_layer(2)
         finish(1)

@@ -35,7 +35,7 @@ def tile_list_pnet_gate_kernel(
         work = ctx.enter_context(tc.tile_pool(name="work", bufs=1))
         psum = ctx.enter_context(tc.psum_pool(name="psum", bufs=1))
 
-        LAP = 64
+        LAP = 256
         RAW = 4096
         at = {}
         at["gate"] = 0
@@ -73,10 +73,10 @@ def tile_list_pnet_gate_kernel(
 
         def tile(name, shape, dtype):
             if name in at:
-                return work.tile(shape, dtype, name=name, align_bytes=64, offset=at[name])
-            return keep.tile(shape, dtype, name=name, align_bytes=64)
+                return work.tile(shape, dtype, name=name, align_bytes=256, offset=at[name])
+            return keep.tile(shape, dtype, name=name, align_bytes=256)
 
-        offsets = keep.tile([P, G * LIST_COLS], U16, name="offsets")
+        offsets = keep.tile([P, G * LIST_COLS], U16, name="offsets", align_bytes=256)
         nc.sync.dma_start(offsets[:], offs)
 
         scale_rows = tile("rows", [P, T // 4], I32)

@@ -42,13 +42,8 @@ def tile_list_pnet_gate_kernel(
         at["c00"] = at["gate"] + 8192 - LAP
         at["rows"] = at["c00"] + RAW - LAP
         at["w1b"] = at["rows"] + RAW - LAP
-        at["picked3"] = at["w1b"] + RAW - LAP
-        at["wc_codes"] = at["picked3"] + LAP
-        at["c_bf0"] = at["picked3"] + 2048
-        at["c_bf1"] = at["c_bf0"] + LAP
-        at["summed1"] = at["c_bf1"]
-        at["summed3"] = at["summed1"]
-        at["w0a"] = at["c_bf1"] + RAW
+        at["words3"] = at["w1b"] + LAP
+        at["w0a"] = at["w1b"] + RAW
         at["c01"] = at["w0a"] + RAW - LAP
         at["first"] = at["c01"] + RAW - LAP
         at["wc_raw"] = at["first"] + 8192 + 2048
@@ -68,8 +63,13 @@ def tile_list_pnet_gate_kernel(
         at["mid11"] = at["mid10"] + 2048
         at["w0b"] = at["mid11"] + 2048
         at["late_rows"] = at["w0b"]
-        at["words1"] = at["w0b"] + 1536
-        at["picked2"] = at["w0b"] + RAW - LAP
+        at["picked2"] = at["w0b"] + 1536
+        at["picked3"] = at["w0b"] + RAW - LAP
+        at["wc_codes"] = at["picked3"] + LAP
+        at["c_bf0"] = at["picked3"] + 2048
+        at["c_bf1"] = at["c_bf0"] + LAP
+        at["summed1"] = at["c_bf1"]
+        at["summed3"] = at["summed1"]
 
         def tile(name, shape, dtype):
             if name in at:
@@ -177,6 +177,7 @@ def tile_list_pnet_gate_kernel(
         pick(0)
         pick(1)
         part_passes(0)
+        part_passes(1)
         quantize_w(0)
         late_rows = tile("late_rows", [P, (2 * J + R) // 4], I32)
         nc.vector.tensor_copy(late_rows[:, 0 : 2 * J // 4], picked_scales[1][:].bitcast(I32))
@@ -189,10 +190,9 @@ def tile_list_pnet_gate_kernel(
         wc_raw = tile("wc_raw", [P, PASSES, R // 2], I32)
         nc.sync.dma_start(wc_raw[:], wc_words.rearrange("a p b -> p a b").bitcast(I32))
         pick(2)
-        part_passes(1)
+        pick(3)
         part_passes(2)
         quantize_w(1)
-        pick(3)
         part_passes(3)
 
         c_codes = [tile(f"c_codes{half}", [P, PASSES, HALF], U32) for half in range(2)]

@@ -24,6 +24,8 @@ PASSES = K // K_PASS
 HALF = 256
 CHUNK = 128
 LIST_COLS = J // 16
+LAP = 256
+PIECE = 4096
 
 
 def tile_list_pnet_gate_kernel(
@@ -35,41 +37,39 @@ def tile_list_pnet_gate_kernel(
         work = ctx.enter_context(tc.tile_pool(name="work", bufs=1))
         psum = ctx.enter_context(tc.psum_pool(name="psum", bufs=1))
 
-        LAP = 256
-        RAW = 4096
         at = {}
-        at["gate"] = 0
-        at["c00"] = at["gate"] + 8192 - LAP
-        at["rows"] = at["c00"] + RAW - LAP
-        at["w1b"] = at["rows"] + RAW - LAP
-        at["words3"] = at["w1b"] + LAP
-        at["w0a"] = at["w1b"] + RAW
-        at["c01"] = at["w0a"] + RAW - LAP
-        at["first"] = at["c01"] + RAW - LAP
-        at["wc_raw"] = at["first"] + 8192 + 2048
-        at["picked_scales1"] = at["wc_raw"] + 2048 - LAP
-        at["c10"] = at["picked_scales1"] + 1024 - LAP
-        at["wd_bf"] = at["c10"] + LAP - RAW
-        at["summed2"] = at["wd_bf"]
-        at["own_sb"] = at["c10"] + LAP
-        at["h_bf2"] = at["own_sb"]
-        at["h_codes0"] = at["h_bf2"] + 1024
-        at["wd_codes"] = at["own_sb"] + 2048 - LAP
-        at["wd_raw"] = at["wd_codes"] + 2048
-        at["w1a"] = at["wd_raw"] + 8192 - LAP
-        at["c11"] = at["w1a"] + RAW - LAP
-        at["summed0"] = at["c11"] + LAP - 2048
-        at["mid10"] = at["c11"] + LAP
+        at["w1_raw"] = 0
+        at["picked3"] = at["w1_raw"]
+        at["words2"] = at["picked3"] + 2048
+        at["rows"] = at["w1_raw"] + 2 * PIECE - LAP
+        at["c0_raw"] = at["rows"] + PIECE - LAP
+        at["first"] = at["c0_raw"] + LAP
+        at["pooled0"] = at["first"] + 2 * PIECE
+        at["c1_raw"] = at["pooled0"] + PIECE - LAP
+        at["picked_scales1"] = at["c1_raw"] + LAP - 1024
+        at["wc_raw"] = at["picked_scales1"] + LAP - 2048
+        at["mid10"] = at["c1_raw"] + LAP
         at["mid11"] = at["mid10"] + 2048
-        at["w0b"] = at["mid11"] + 2048
-        at["late_rows"] = at["w0b"]
-        at["picked2"] = at["w0b"] + 1536
-        at["picked3"] = at["w0b"] + RAW - LAP
-        at["wc_codes"] = at["picked3"] + LAP
-        at["c_bf0"] = at["picked3"] + 2048
-        at["c_bf1"] = at["c_bf0"] + LAP
-        at["summed1"] = at["c_bf1"]
-        at["summed3"] = at["summed1"]
+        at["own_sb0"] = at["mid11"] + 2048
+        at["own_sb1"] = at["own_sb0"] + 2048
+        at["wd_codes"] = at["own_sb1"] + LAP - 2048
+        at["h_bf2"] = at["own_sb1"] + LAP
+        at["summed3"] = at["h_bf2"] + 1024
+        at["table"] = at["summed3"] + 2048
+        at["wd_raw"] = at["table"]
+        at["gate"] = at["wd_raw"] + 2 * PIECE
+        for ch in (0, 1, 3):
+            at[f"h_bf{ch}"] = at["wd_raw"] + 1024 * ch
+        at["words1"] = at["table"] + 4 * PIECE
+        at["c1_bf"] = at["words1"]
+        at["w0b_raw"] = at["words1"] + 2048 - LAP
+        at["picked2"] = at["w0b_raw"] + LAP
+        at["late_rows"] = at["picked2"] + 2048
+        at["wc_codes"] = at["w0b_raw"] + PIECE
+        at["c0_bf"] = at["wc_codes"] + 2048 - LAP
+        at["summed2"] = at["c0_bf"] + PIECE
+        at["res0"] = at["summed2"]
+        at["res1"] = at["summed3"]
 
         def tile(name, shape, dtype):
             if name in at:
@@ -86,29 +86,26 @@ def tile_list_pnet_gate_kernel(
         table = tile("table", [P, T], I32)
         nc.sync.dma_start(table[:], tab_words[0].rearrange("p t b -> p (t b)").bitcast(I32))
 
-        wcs_rows = tile("wcs_rows", [P, R // 4], I32)
-        nc.sync.dma_start(wcs_rows[96:128, :], wc_scales.rearrange("a q n -> q a n").bitcast(I32))
-        nc.vector.memset(wcs_rows[0:96, :], 0)
+        wcs_raw = tile("wcs_raw", [P, R // 4], I32)
+        nc.sync.dma_start(wcs_raw[96:128, :], wc_scales.rearrange("a q n -> q a n").bitcast(I32))
+        nc.vector.memset(wcs_raw[0:96, :], 0)
 
-        early_planes = tile("early_planes", [P, PASSES, 2 * J // 4], I32)
-        nc.gpsimd.memset(early_planes[:], 0)
-        late_planes = tile("late_planes", [P, PASSES, (2 * J + R) // 4], I32)
-        nc.gpsimd.memset(late_planes[:], 0)
+        tab_planes = []
+        for s, width in enumerate((2 * J, 2 * J + R)):
+            tab_planes.append(tile(f"tab_planes{s}", [P, PASSES, width // 4], I32))
+            nc.gpsimd.memset(tab_planes[s][:], 0)
 
-        def load_half(src, a, half, name):
-            raw = tile(name, [P, PACK, HALF], F32)
+        def load_piece(raw, src, a, half):
             rows = src[a * K_PASS : (a + 1) * K_PASS, half * HALF : (half + 1) * HALF]
-            nc.sync.dma_start(raw[:], rows.rearrange("(p j) x -> p j x", j=PACK))
-            return raw
+            nc.sync.dma_start(raw, rows.rearrange("(p j) x -> p j x", j=PACK))
 
         w_codes = tile("w_codes", [P, PASSES, R], U32)
         w_scales = tile("w_scales", [P, PASSES, R], U8)
         w_bfs = [tile(f"w_bf{a}", [P, R * PACK], BF16) for a in range(PASSES)]
 
-        def cast_w(a, half):
-            raw = load_half(w, a, half, f"w{a}{'ab'[half]}")
+        def cast_w(raw, a, half):
             dst = w_bfs[a][:].rearrange("p (t h i j) -> p h t j i", t=4, i=4, j=PACK)
-            src = raw[:].rearrange("p j (h t i) -> p h t j i", t=4, i=4)
+            src = raw.rearrange("p j (h t i) -> p h t j i", t=4, i=4)
             part = dst[:, 16 * half : 16 * half + 16]
             if a == 0 and half == 0:
                 nc.scalar.activation(part[:, :, 0], src[:, :, 0], ACT.Copy)
@@ -119,16 +116,18 @@ def tile_list_pnet_gate_kernel(
                 for t in (0, 2):
                     nc.scalar.copy(part[:, :, t : t + 2], src[:, :, t : t + 2])
 
-        def quantize_w(a):
-            for x in (0, HALF):
-                nc.vector.quantize_mx(
-                    w_codes[:, a, x : x + HALF].bitcast(FP8X4),
-                    w_scales[:, a, x : x + HALF],
-                    w_bfs[a][:, PACK * x : PACK * (x + HALF)],
-                )
+        def quantize_w(a, pair):
+            x = pair * HALF
+            nc.vector.quantize_mx(
+                w_codes[:, a, x : x + HALF].bitcast(FP8X4),
+                w_scales[:, a, x : x + HALF],
+                w_bfs[a][:, PACK * x : PACK * (x + HALF)],
+            )
 
-        cast_w(0, 0)
-        cast_w(0, 1)
+        for half in range(2):
+            raw = tile(f"w0{'ab'[half]}_raw", [P, PACK, HALF], F32)
+            load_piece(raw[:], w, 0, half)
+            cast_w(raw[:], 0, half)
 
         picked_scales = []
         for s in range(2):
@@ -142,20 +141,24 @@ def tile_list_pnet_gate_kernel(
             for q in (0, 2, 1, 3):
                 nc.sync.dma_start(planes[32 * q : 32 * q + 4], rows[96 + 8 * q : 96 + 8 * q + 8, :])
 
-        move_rows(early_planes, picked_scales[0][:].bitcast(I32))
-        cast_w(1, 0)
-        cast_w(1, 1)
+        move_rows(tab_planes[0], picked_scales[0][:].bitcast(I32))
 
-        def cast_c(dst, a, half):
-            raw = load_half(c, a, half, f"c{half}{a}")
+        w1_raw = tile("w1_raw", [P, 2, PACK, HALF], F32)
+        for half in range(2):
+            load_piece(w1_raw[:, half], w, 1, half)
+            cast_w(w1_raw[:, half], 1, half)
+
+        def cast_c(dst, raw):
             nc.scalar.copy(
                 dst.rearrange("p (x i j) -> p x j i", i=4, j=PACK),
-                raw[:].rearrange("p j (x i) -> p x j i", i=4),
+                raw.rearrange("p j (x i) -> p x j i", i=4),
             )
 
-        c_bf0 = tile("c_bf0", [P, PASSES, HALF * PACK], BF16)
+        c0_raw = tile("c0_raw", [P, PASSES, PACK, HALF], F32)
+        c0_bf = tile("c0_bf", [P, PASSES, HALF * PACK], BF16)
         for a in range(PASSES):
-            cast_c(c_bf0[:, a, :], a, 0)
+            load_piece(c0_raw[:, a], c, a, 0)
+            cast_c(c0_bf[:, a, :], c0_raw[:, a])
 
         parted = {}
         picked = {}
@@ -177,35 +180,41 @@ def tile_list_pnet_gate_kernel(
         pick(0)
         pick(1)
         part_passes(0)
+        quantize_w(0, 0)
         part_passes(1)
-        quantize_w(0)
+        quantize_w(0, 1)
         late_rows = tile("late_rows", [P, (2 * J + R) // 4], I32)
-        nc.vector.tensor_copy(late_rows[:, 0 : 2 * J // 4], picked_scales[1][:].bitcast(I32))
         nc.vector.tensor_copy(
             late_rows[:, 2 * J // 4 :].rearrange("p (t h) -> p t h", t=4),
-            wcs_rows[:].rearrange("p (h t) -> p t h", t=4),
+            wcs_raw[:, :].rearrange("p (h t) -> p t h", t=4),
         )
-        move_rows(late_planes, late_rows)
-        tab_planes = [early_planes[:].bitcast(U8), late_planes[:].bitcast(U8)]
+        nc.vector.tensor_copy(late_rows[:, 0 : 2 * J // 4], picked_scales[1][:, :].bitcast(I32))
+
+        move_rows(tab_planes[1], late_rows)
         wc_raw = tile("wc_raw", [P, PASSES, R // 2], I32)
         nc.sync.dma_start(wc_raw[:], wc_words.rearrange("a p b -> p a b").bitcast(I32))
+        c1_raw = tile("c1_raw", [P, PASSES, PACK, HALF], F32)
+        for a in range(PASSES):
+            load_piece(c1_raw[:, a], c, a, 1)
+
         pick(2)
+        quantize_w(1, 0)
         pick(3)
+        quantize_w(1, 1)
         part_passes(2)
-        quantize_w(1)
         part_passes(3)
 
-        c_codes = [tile(f"c_codes{half}", [P, PASSES, HALF], U32) for half in range(2)]
+        c_codes = tile("c_codes", [P, 2, PASSES, HALF], U32)
         c_scales = tile("c_scales", [P, 2, PASSES, HALF], U8)
 
         def quantize_c(half, c_bf):
             nc.vector.quantize_mx(
-                c_codes[half][:].rearrange("p a x -> p (a x)").bitcast(FP8X4),
+                c_codes[:, half].rearrange("p a x -> p (a x)").bitcast(FP8X4),
                 c_scales[:, half].rearrange("p a x -> p (a x)"),
                 c_bf[:].rearrange("p a x -> p (a x)"),
             )
 
-        quantize_c(0, c_bf0)
+        quantize_c(0, c0_bf)
 
         wc_codes = tile("wc_codes", [P, PASSES, R // 2], I32)
         nc.gpsimd.tensor_copy(
@@ -213,25 +222,31 @@ def tile_list_pnet_gate_kernel(
             wc_raw[:].rearrange("p a (h t x) -> p a t h x", t=4, x=2),
         )
 
+        wd_raw = tile("wd_raw", [P, PACK, N], F32)
+        wd_rows = wd.rearrange("(h t i) n -> t h i n", t=4, i=4)
+        for t in range(4):
+            nc.sync.dma_start(wd_raw[:, t, :], wd_rows[t])
+        gate = tile("gate", [P, 4, J], F32)
+        nc.sync.dma_start(gate[:], gm.rearrange("(u p) j -> p u j", p=P))
+
         def project(dst, g, t, a, j0, width):
+            plane = tab_planes[g // 2][:].bitcast(U8)
             nc.tensor.matmul_mx(
                 out=dst,
                 lhsT=w_codes[:, a, t * P : (t + 1) * P].bitcast(FP8X4),
                 lhsT_scale=w_scales[:, a, t * P : (t + 1) * P],
                 rhs=parted[g][:, a, 2 * j0 : 2 * (j0 + width)].bitcast(FP4X4),
-                rhs_scale=tab_planes[g // 2][:, a, g % 2 * J + j0 : g % 2 * J + j0 + width],
+                rhs_scale=plane[:, a, g % 2 * J + j0 : g % 2 * J + j0 + width],
                 start=(a == 0),
                 stop=(a == PASSES - 1),
             )
 
         banks = [[psum.tile([P, J], F32, name=f"a{g}_{t}", tag=f"bank{4 * g + t}") for t in range(4)] for g in range(2)]
-        for g in range(2):
-            for t in range(4):
-                project(banks[g][t][:], g, t, 0, 0, J)
-        for t0 in (0, 2):
-            for g in range(2):
-                for t in (t0, t0 + 1):
-                    project(banks[g][t][:], g, t, 1, 0, J)
+        for a in range(PASSES):
+            for t0 in (0, 2):
+                for g in range(2):
+                    for t in (t0, t0 + 1):
+                        project(banks[g][t][:], g, t, a, 0, J)
 
         first = tile("first", [P, 4, J], F32)
         best = tile("best", [P, 4, J], F32)
@@ -240,15 +255,9 @@ def tile_list_pnet_gate_kernel(
         for t in range(4):
             nc.vector.tensor_tensor(best[:, t, :], banks[1][t][:], first[:, t, :], ALU.max)
 
-        c_bf1 = tile("c_bf1", [P, PASSES, HALF * PACK], BF16)
+        c1_bf = tile("c1_bf", [P, PASSES, HALF * PACK], BF16)
         for a in range(PASSES):
-            cast_c(c_bf1[:, a, :], a, 1)
-        wd_raw = tile("wd_raw", [P, PACK, N], F32)
-        wd_rows = wd.rearrange("(h t i) n -> t h i n", t=4, i=4)
-        for t in range(4):
-            nc.sync.dma_start(wd_raw[:, t, :], wd_rows[t])
-        gate = tile("gate", [P, 4, J], F32)
-        nc.sync.dma_start(gate[:], gm.rearrange("(u p) j -> p u j", p=P))
+            cast_c(c1_bf[:, a, :], c1_raw[:, a])
 
         late = {}
 
@@ -260,7 +269,7 @@ def tile_list_pnet_gate_kernel(
             late[g, half, pair] = bank
 
         wc_bytes = wc_codes[:].bitcast(U8)
-        wc_scale_bytes = tab_planes[1][:, :, 2 * J :]
+        wc_scale_bytes = tab_planes[1][:].bitcast(U8)[:, :, 2 * J :]
 
         owns = {}
 
@@ -273,14 +282,13 @@ def tile_list_pnet_gate_kernel(
                         out=owns[ch][:, t, :],
                         lhsT=wc_bytes[:, a, 2 * t * P : 2 * (t + 1) * P].bitcast(FP4X4),
                         lhsT_scale=wc_scale_bytes[:, a, t * P : (t + 1) * P],
-                        rhs=c_codes[half][:, a, x0 : x0 + CHUNK].bitcast(FP8X4),
+                        rhs=c_codes[:, half, a, x0 : x0 + CHUNK].bitcast(FP8X4),
                         rhs_scale=c_scales[:, half, a, x0 : x0 + CHUNK],
                         start=(a == 0),
                         stop=(a == PASSES - 1),
                     )
 
         mid = {}
-        pooled = [tile(f"pooled{half}", [P, 2, 4, CHUNK], F32) for half in range(2)]
 
         def pool_mid(half, pair):
             cols = slice(half * HALF, (half + 1) * HALF)
@@ -289,44 +297,51 @@ def tile_list_pnet_gate_kernel(
                 mid[half, pair][:], late[2, half, pair][:], best[:, 2 * pair : 2 * pair + 2, cols], ALU.max
             )
 
-        def pool_last(half, pair):
-            nc.vector.tensor_tensor(
-                pooled[half][:, :, 2 * pair : 2 * pair + 2, :],
-                late[3, half, pair][:].rearrange("p t (c x) -> p c t x", c=2),
-                mid[half, pair][:].rearrange("p t (c x) -> p c t x", c=2),
-                ALU.max,
-            )
-
         for g in (2, 3):
             for pair in range(2):
                 project_late(g, 0, pair, f"bank{2 * (g - 2) + pair}")
-        pool_mid(0, 0)
-        pool_mid(0, 1)
-        project_own(1, "bank4")
-        project_own(0, "bank5")
-        own_sb = tile("own_sb", [P, 4, CHUNK], F32)
-        nc.scalar.copy(own_sb[:], owns[1][:])
+        for ch in range(2):
+            project_own(ch, f"bank{4 + ch}")
         for pair in range(2):
-            project_late(2, 1, pair, f"bank{pair}")
+            pool_mid(0, pair)
+        quantize_c(1, c1_bf)
+        pooled0 = tile("pooled0", [P, 2, 4, CHUNK], F32)
         for pair in range(2):
-            pool_last(0, pair)
-        quantize_c(1, c_bf1)
-        for pair in range(2):
-            project_late(3, 1, pair, f"bank{2 + pair}")
+            nc.vector.tensor_tensor(
+                pooled0[:, :, 2 * pair : 2 * pair + 2, :],
+                late[3, 0, pair][:].rearrange("p t (c x) -> p c t x", c=2),
+                mid[0, pair][:].rearrange("p t (c x) -> p c t x", c=2),
+                ALU.max,
+            )
+        summed = {}
+        for ch in range(2):
+            own_sb = tile(f"own_sb{ch}", [P, 4, CHUNK], F32)
+            nc.scalar.copy(own_sb[:], owns[ch][:])
+            summed[ch] = tile(f"summed{ch}", [P, 4, CHUNK], F32)
+            nc.gpsimd.tensor_tensor(summed[ch][:], own_sb[:], pooled0[:, ch], ALU.add)
+        for g in (2, 3):
+            for pair in range(2):
+                project_late(g, 1, pair, f"bank{2 * (g - 2) + pair}")
         project_own(2, "bank6")
-        project_own(3, "bank7")
-        summed = {1: tile("summed1", [P, 4, CHUNK], F32)}
-        nc.gpsimd.tensor_tensor(summed[1][:], own_sb[:], pooled[0][:, 1], ALU.add)
+        for pair in range(2):
+            pool_mid(1, pair)
+        pooled1 = tile("pooled1", [P, 2, 4, CHUNK], F32)
+        for ch in range(2):
+            cols = slice(ch * CHUNK, (ch + 1) * CHUNK)
+            for pair in range(2):
+                nc.vector.tensor_tensor(
+                    pooled1[:, ch, 2 * pair : 2 * pair + 2, :],
+                    late[3, 1, pair][:, :, cols],
+                    mid[1, pair][:, :, cols],
+                    ALU.max,
+                )
+        project_own(3, "bank2")
 
         def add_own(ch):
             summed[ch] = tile(f"summed{ch}", [P, 4, CHUNK], F32)
-            nc.vector.tensor_tensor(summed[ch][:], owns[ch][:], pooled[ch // 2][:, ch % 2], ALU.add)
+            nc.vector.tensor_tensor(summed[ch][:], owns[ch][:], pooled1[:, ch - 2], ALU.add)
 
-        add_own(0)
-        for pair in range(2):
-            pool_mid(1, pair)
-        for pair in range(2):
-            pool_last(1, pair)
+        add_own(2)
 
         wd_bf = tile("wd_bf", [P, N * PACK], BF16)
         for half in range(2):
@@ -334,6 +349,9 @@ def tile_list_pnet_gate_kernel(
                 wd_bf[:, half * HALF * PACK : (half + 1) * HALF * PACK].rearrange("p (x i t) -> p x t i", i=4, t=PACK),
                 wd_raw[:, :, half * HALF : (half + 1) * HALF].rearrange("p t (x i) -> p x t i", i=4),
             )
+        wd_codes = tile("wd_codes", [P, N], U32)
+        wd_scales = tile("wd_scales", [P, N], U8)
+        nc.vector.quantize_mx(wd_codes[:].bitcast(FP8X4), wd_scales[:], wd_bf[:])
 
         h_bf = {}
 
@@ -345,21 +363,14 @@ def tile_list_pnet_gate_kernel(
                 ACT.Relu,
             )
 
-        relu(0)
-        relu(1)
-        wd_codes = tile("wd_codes", [P, N], U32)
-        wd_scales = tile("wd_scales", [P, N], U8)
-        nc.vector.quantize_mx(wd_codes[:].bitcast(FP8X4), wd_scales[:], wd_bf[:])
-
         out_rows = out.rearrange("(u p) j -> p u j", p=P)
-
         ys = {}
 
         def second_layer(ch):
             h_codes = tile(f"h_codes{ch}", [P, CHUNK], U32)
             h_scales = tile(f"h_scales{ch}", [P, CHUNK], U8)
             nc.vector.quantize_mx(h_codes[:].bitcast(FP8X4), h_scales[:], h_bf[ch][:])
-            ys[ch] = psum.tile([P, 4, CHUNK], F32, name=f"y{ch}", tag=f"bank{(4 + ch) % 6}")
+            ys[ch] = psum.tile([P, 4, CHUNK], F32, name=f"y{ch}", tag=f"bank{(4, 5, 7, 0)[ch]}")
             for u in range(4):
                 nc.tensor.matmul_mx(
                     out=ys[ch][:, u, :],
@@ -380,15 +391,16 @@ def tile_list_pnet_gate_kernel(
                 nc.vector.tensor_tensor(res[:, us, :], ys[ch][:, us, :], gate[:, us, cols], ALU.mult)
                 nc.sync.dma_start(out_rows[:, us, cols], res[:, us, :])
 
+        relu(0)
         second_layer(0)
-        add_own(2)
-        relu(2)
-        second_layer(1)
         add_own(3)
-        relu(3)
-        finish(0)
+        relu(1)
+        second_layer(1)
+        relu(2)
         second_layer(2)
-        finish(1)
+        finish(0)
+        relu(3)
         second_layer(3)
+        finish(1)
         finish(2)
         finish(3)

@@ -297,6 +297,17 @@ def tile_list_pnet_gate_kernel(
                 mid[half, pair][:], late[2, half, pair][:], best[:, 2 * pair : 2 * pair + 2, cols], ALU.max
             )
 
+        def pool_last(pooled, half):
+            for ch in range(2):
+                cols = slice(ch * CHUNK, (ch + 1) * CHUNK)
+                for pair in range(2):
+                    nc.vector.tensor_tensor(
+                        pooled[:, ch, 2 * pair : 2 * pair + 2, :],
+                        late[3, half, pair][:, :, cols],
+                        mid[half, pair][:, :, cols],
+                        ALU.max,
+                    )
+
         for g in (2, 3):
             for pair in range(2):
                 project_late(g, 0, pair, f"bank{2 * (g - 2) + pair}")
@@ -306,13 +317,7 @@ def tile_list_pnet_gate_kernel(
             pool_mid(0, pair)
         quantize_c(1, c1_bf)
         pooled0 = tile("pooled0", [P, 2, 4, CHUNK], F32)
-        for pair in range(2):
-            nc.vector.tensor_tensor(
-                pooled0[:, :, 2 * pair : 2 * pair + 2, :],
-                late[3, 0, pair][:].rearrange("p t (c x) -> p c t x", c=2),
-                mid[0, pair][:].rearrange("p t (c x) -> p c t x", c=2),
-                ALU.max,
-            )
+        pool_last(pooled0, 0)
         summed = {}
         for ch in range(2):
             own_sb = tile(f"own_sb{ch}", [P, 4, CHUNK], F32)
@@ -326,15 +331,7 @@ def tile_list_pnet_gate_kernel(
         for pair in range(2):
             pool_mid(1, pair)
         pooled1 = tile("pooled1", [P, 2, 4, CHUNK], F32)
-        for ch in range(2):
-            cols = slice(ch * CHUNK, (ch + 1) * CHUNK)
-            for pair in range(2):
-                nc.vector.tensor_tensor(
-                    pooled1[:, ch, 2 * pair : 2 * pair + 2, :],
-                    late[3, 1, pair][:, :, cols],
-                    mid[1, pair][:, :, cols],
-                    ALU.max,
-                )
+        pool_last(pooled1, 1)
         project_own(3, "bank2")
 
         def add_own(ch):
@@ -393,9 +390,9 @@ def tile_list_pnet_gate_kernel(
 
         relu(0)
         second_layer(0)
-        add_own(3)
         relu(1)
         second_layer(1)
+        add_own(3)
         relu(2)
         second_layer(2)
         finish(0)

@@ -93,7 +93,8 @@ def tile_list_pnet_gate_kernel(
         tab_planes = []
         for s, width in enumerate((2 * J, 2 * J + R)):
             tab_planes.append(tile(f"tab_planes{s}", [P, PASSES, width // 4], I32))
-            nc.gpsimd.memset(tab_planes[s][:], 0)
+        nc.vector.memset(tab_planes[0][:], 0)
+        nc.gpsimd.memset(tab_planes[1][:], 0)
 
         def load_piece(raw, src, a, half):
             rows = src[a * K_PASS : (a + 1) * K_PASS, half * HALF : (half + 1) * HALF]

@@ -62,8 +62,8 @@ def tile_list_pnet_gate_kernel(
             at[f"h_bf{ch}"] = at["wd_raw"] + 1024 * ch
         at["words1"] = at["table"] + 4 * PIECE
         at["c1_bf"] = at["words1"]
-        at["w0b_raw"] = at["words1"] + 2048 - LAP
-        at["picked2"] = at["w0b_raw"] + LAP
+        at["w0b_raw"] = at["words1"] + 2048
+        at["picked2"] = at["w0b_raw"]
         at["late_rows"] = at["picked2"] + 2048
         at["wc_codes"] = at["w0b_raw"] + PIECE
         at["c0_bf"] = at["wc_codes"] + 2048 - LAP
@@ -181,8 +181,8 @@ def tile_list_pnet_gate_kernel(
         pick(0)
         pick(1)
         part_passes(0)
-        quantize_w(0, 0)
         part_passes(1)
+        quantize_w(0, 0)
         quantize_w(0, 1)
         late_rows = tile("late_rows", [P, (2 * J + R) // 4], I32)
         nc.vector.tensor_copy(

from contextlib import ExitStack

import concourse.mybir as mybir

K, R, N, T, J = 1024, 512, 512, 4096, 512
G = 4
FLOPS = 2 * (G + 1) * K * R * J + 2 * R * N * J

F32 = mybir.dt.float32
BF16 = mybir.dt.bfloat16
I32 = mybir.dt.int32
U32 = mybir.dt.uint32
U16 = mybir.dt.uint16
U8 = mybir.dt.uint8
FP8X4 = mybir.dt.float8_e4m3fn_x4
FP4X4 = mybir.dt.float4_e2m1fn_x4
ACT = mybir.ActivationFunctionType
ALU = mybir.AluOpType

P = 128
PACK = 4
K_PASS = P * PACK
PASSES = K // K_PASS
HALF = 256
CHUNK = 128
LIST_COLS = J // 16
LAP = 256
PIECE = 4096


def tile_list_pnet_gate_kernel(
    tc, tab_words, tab_scales, c, w, wc_words, wc_scales, wd, gm, offs, out
):
    nc = tc.nc
    with ExitStack() as ctx:
        keep = ctx.enter_context(tc.tile_pool(name="keep", bufs=1))
        work = ctx.enter_context(tc.tile_pool(name="work", bufs=1))
        psum = ctx.enter_context(tc.psum_pool(name="psum", bufs=1))

        at = {}
        at["w1_raw"] = 0
        at["picked3"] = at["w1_raw"]
        at["words2"] = at["picked3"] + 2048
        at["rows"] = at["w1_raw"] + 2 * PIECE - LAP
        at["c0_raw"] = at["rows"] + PIECE - LAP
        at["first"] = at["c0_raw"] + LAP
        at["pooled0"] = at["first"] + 2 * PIECE
        at["c1_raw"] = at["pooled0"] + PIECE - LAP
        at["picked_scales1"] = at["c1_raw"] + LAP - 1024
        at["wc_raw"] = at["picked_scales1"] + LAP - 2048
        at["mid10"] = at["c1_raw"] + LAP
        at["mid11"] = at["mid10"] + 2048
        at["own_sb0"] = at["mid11"] + 2048
        at["own_sb1"] = at["own_sb0"] + 2048
        at["wd_codes"] = at["own_sb1"] + LAP - 2048
        at["h_bf2"] = at["own_sb1"] + LAP
        at["summed3"] = at["h_bf2"] + 1024
        at["table"] = at["summed3"] + 2048
        at["wd_raw"] = at["table"]
        at["gate"] = at["wd_raw"] + 2 * PIECE
        for ch in (0, 1, 3):
            at[f"h_bf{ch}"] = at["wd_raw"] + 1024 * ch
        at["words1"] = at["table"] + 4 * PIECE
        at["c1_bf"] = at["words1"]
        at["w0b_raw"] = at["words1"] + 2048
        at["picked2"] = at["w0b_raw"]
        at["late_rows"] = at["picked2"] + 2048
        at["wc_codes"] = at["w0b_raw"] + PIECE
        at["c0_bf"] = at["wc_codes"] + 2048 - LAP
        at["summed2"] = at["c0_bf"] + PIECE
        at["res0"] = at["summed2"]
        at["res1"] = at["summed3"]

        def tile(name, shape, dtype):
            if name in at:
                return work.tile(shape, dtype, name=name, align_bytes=256, offset=at[name])
            return keep.tile(shape, dtype, name=name, align_bytes=256)

        offsets = keep.tile([P, G * LIST_COLS], U16, name="offsets", align_bytes=256)
        nc.sync.dma_start(offsets[:], offs)

        scale_rows = tile("rows", [P, T // 4], I32)
        nc.sync.dma_start(scale_rows[96:128, :], tab_scales.rearrange("a q t -> q a t").bitcast(I32))
        nc.vector.memset(scale_rows[0:96, :], 0)

        table = tile("table", [P, T], I32)
        nc.sync.dma_start(table[:], tab_words[0].rearrange("p t b -> p (t b)").bitcast(I32))

        wcs_raw = tile("wcs_raw", [P, R // 4], I32)
        nc.sync.dma_start(wcs_raw[96:128, :], wc_scales.rearrange("a q n -> q a n").bitcast(I32))
        nc.vector.memset(wcs_raw[0:96, :], 0)

        tab_planes = []
        for s, width in enumerate((2 * J, 2 * J + R)):
            tab_planes.append(tile(f"tab_planes{s}", [P, PASSES, width // 4], I32))
        nc.vector.memset(tab_planes[0][:], 0)
        nc.gpsimd.memset(tab_planes[1][:], 0)

        def load_piece(raw, src, a, half):
            rows = src[a * K_PASS : (a + 1) * K_PASS, half * HALF : (half + 1) * HALF]
            nc.sync.dma_start(raw, rows.rearrange("(p j) x -> p j x", j=PACK))

        w_codes = tile("w_codes", [P, PASSES, R], U32)
        w_scales = tile("w_scales", [P, PASSES, R], U8)
        w_bfs = [tile(f"w_bf{a}", [P, R * PACK], BF16) for a in range(PASSES)]

        def cast_w(raw, a, half):
            dst = w_bfs[a][:].rearrange("p (t h i j) -> p h t j i", t=4, i=4, j=PACK)
            src = raw.rearrange("p j (h t i) -> p h t j i", t=4, i=4)
            part = dst[:, 16 * half : 16 * half + 16]
            if a == 0 and half == 0:
                nc.scalar.activation(part[:, :, 0], src[:, :, 0], ACT.Copy)
                nc.scalar.copy(part[:, :, 1:4], src[:, :, 1:4])
            elif half == 0:
                nc.scalar.copy(part, src)
            else:
                for t in (0, 2):
                    nc.scalar.copy(part[:, :, t : t + 2], src[:, :, t : t + 2])

        def quantize_w(a, pair):
            x = pair * HALF
            nc.vector.quantize_mx(
                w_codes[:, a, x : x + HALF].bitcast(FP8X4),
                w_scales[:, a, x : x + HALF],
                w_bfs[a][:, PACK * x : PACK * (x + HALF)],
            )

        for half in range(2):
            raw = tile(f"w0{'ab'[half]}_raw", [P, PACK, HALF], F32)
            load_piece(raw[:], w, 0, half)
            cast_w(raw[:], 0, half)

        picked_scales = []
        for s in range(2):
            picked_scales.append(tile(f"picked_scales{s}", [P, 2 * J], U8))
            nc.vector.tensor_copy(
                picked_scales[s][:],
                scale_rows[:].bitcast(U8).indirect(offsets[:, s * 2 * LIST_COLS : (s + 1) * 2 * LIST_COLS]),
            )

        def move_rows(planes, rows):
            for q in (0, 2, 1, 3):
                nc.sync.dma_start(planes[32 * q : 32 * q + 4], rows[96 + 8 * q : 96 + 8 * q + 8, :])

        move_rows(tab_planes[0], picked_scales[0][:].bitcast(I32))

        w1_raw = tile("w1_raw", [P, 2, PACK, HALF], F32)
        for half in range(2):
            load_piece(w1_raw[:, half], w, 1, half)
            cast_w(w1_raw[:, half], 1, half)

        def cast_c(dst, raw):
            nc.scalar.copy(
                dst.rearrange("p (x i j) -> p x j i", i=4, j=PACK),
                raw.rearrange("p j (x i) -> p x j i", i=4),
            )

        c0_raw = tile("c0_raw", [P, PASSES, PACK, HALF], F32)
        c0_bf = tile("c0_bf", [P, PASSES, HALF * PACK], BF16)
        for a in range(PASSES):
            load_piece(c0_raw[:, a], c, a, 0)
            cast_c(c0_bf[:, a, :], c0_raw[:, a])

        parted = {}
        picked = {}

        def pick(g):
            picked[g] = tile(f"picked{g}", [P, J], U32)
            nc.vector.tensor_copy(
                picked[g][:],
                table[:].bitcast(U32).indirect(offsets[:, g * LIST_COLS : (g + 1) * LIST_COLS]),
            )

        def part_passes(g):
            parted[g] = tile(f"words{g}", [P, PASSES, 2 * J], U8)
            nc.vector.tensor_copy(
                parted[g][:].bitcast(U16).rearrange("p d (h n) -> p h d n", h=2),
                picked[g][:].bitcast(U16).rearrange("p (h n d) -> p h d n", h=2, d=PASSES),
            )

        pick(0)
        pick(1)
        part_passes(0)
        part_passes(1)
        quantize_w(0, 0)
        quantize_w(0, 1)
        late_rows = tile("late_rows", [P, (2 * J + R) // 4], I32)
        nc.vector.tensor_copy(
            late_rows[:, 2 * J // 4 :].rearrange("p (t h) -> p t h", t=4),
            wcs_raw[:, :].rearrange("p (h t) -> p t h", t=4),
        )
        nc.vector.tensor_copy(late_rows[:, 0 : 2 * J // 4], picked_scales[1][:, :].bitcast(I32))

        move_rows(tab_planes[1], late_rows)
        wc_raw = tile("wc_raw", [P, PASSES, R // 2], I32)
        nc.sync.dma_start(wc_raw[:], wc_words.rearrange("a p b -> p a b").bitcast(I32))
        c1_raw = tile("c1_raw", [P, PASSES, PACK, HALF], F32)
        for a in range(PASSES):
            load_piece(c1_raw[:, a], c, a, 1)

        pick(2)
        quantize_w(1, 0)
        pick(3)
        quantize_w(1, 1)
        part_passes(2)
        part_passes(3)

        c_codes = tile("c_codes", [P, 2, PASSES, HALF], U32)
        c_scales = tile("c_scales", [P, 2, PASSES, HALF], U8)

        def quantize_c(half, c_bf):
            nc.vector.quantize_mx(
                c_codes[:, half].rearrange("p a x -> p (a x)").bitcast(FP8X4),
                c_scales[:, half].rearrange("p a x -> p (a x)"),
                c_bf[:].rearrange("p a x -> p (a x)"),
            )

        quantize_c(0, c0_bf)

        wc_codes = tile("wc_codes", [P, PASSES, R // 2], I32)
        nc.gpsimd.tensor_copy(
            wc_codes[:].rearrange("p a (t h x) -> p a t h x", t=4, x=2),
            wc_raw[:].rearrange("p a (h t x) -> p a t h x", t=4, x=2),
        )

        wd_raw = tile("wd_raw", [P, PACK, N], F32)
        wd_rows = wd.rearrange("(h t i) n -> t h i n", t=4, i=4)
        for t in range(4):
            nc.sync.dma_start(wd_raw[:, t, :], wd_rows[t])
        gate = tile("gate", [P, 4, J], F32)
        nc.sync.dma_start(gate[:], gm.rearrange("(u p) j -> p u j", p=P))

        def project(dst, g, t, a, j0, width):
            plane = tab_planes[g // 2][:].bitcast(U8)
            nc.tensor.matmul_mx(
                out=dst,
                lhsT=w_codes[:, a, t * P : (t + 1) * P].bitcast(FP8X4),
                lhsT_scale=w_scales[:, a, t * P : (t + 1) * P],
                rhs=parted[g][:, a, 2 * j0 : 2 * (j0 + width)].bitcast(FP4X4),
                rhs_scale=plane[:, a, g % 2 * J + j0 : g % 2 * J + j0 + width],
                start=(a == 0),
                stop=(a == PASSES - 1),
            )

        banks = [[psum.tile([P, J], F32, name=f"a{g}_{t}", tag=f"bank{4 * g + t}") for t in range(4)] for g in range(2)]
        for a in range(PASSES):
            for t0 in (0, 2):
                for g in range(2):
                    for t in (t0, t0 + 1):
                        project(banks[g][t][:], g, t, a, 0, J)

        first = tile("first", [P, 4, J], F32)
        best = tile("best", [P, 4, J], F32)
        for t in range(4):
            nc.scalar.copy(first[:, t, :], banks[0][t][:])
        for t in range(4):
            nc.vector.tensor_tensor(best[:, t, :], banks[1][t][:], first[:, t, :], ALU.max)

        c1_bf = tile("c1_bf", [P, PASSES, HALF * PACK], BF16)
        for a in range(PASSES):
            cast_c(c1_bf[:, a, :], c1_raw[:, a])

        late = {}

        def project_late(g, half, pair, tag):
            bank = psum.tile([P, 2, HALF], F32, name=f"a{g}_{half}{pair}", tag=tag)
            for k in range(2):
                for a in range(PASSES):
                    project(bank[:, k, :], g, 2 * pair + k, a, half * HALF, HALF)
            late[g, half, pair] = bank

        wc_bytes = wc_codes[:].bitcast(U8)
        wc_scale_bytes = tab_planes[1][:].bitcast(U8)[:, :, 2 * J :]

        owns = {}

        def project_own(ch, tag):
            half, x0 = divmod(ch * CHUNK, HALF)
            owns[ch] = psum.tile([P, 4, CHUNK], F32, name=f"own{ch}", tag=tag)
            for t in range(4):
                for a in range(PASSES):
                    nc.tensor.matmul_mx(
                        out=owns[ch][:, t, :],
                        lhsT=wc_bytes[:, a, 2 * t * P : 2 * (t + 1) * P].bitcast(FP4X4),
                        lhsT_scale=wc_scale_bytes[:, a, t * P : (t + 1) * P],
                        rhs=c_codes[:, half, a, x0 : x0 + CHUNK].bitcast(FP8X4),
                        rhs_scale=c_scales[:, half, a, x0 : x0 + CHUNK],
                        start=(a == 0),
                        stop=(a == PASSES - 1),
                    )

        mid = {}

        def pool_mid(half, pair):
            cols = slice(half * HALF, (half + 1) * HALF)
            mid[half, pair] = tile(f"mid{half}{pair}", [P, 2, HALF], F32)
            nc.vector.tensor_tensor(
                mid[half, pair][:], late[2, half, pair][:], best[:, 2 * pair : 2 * pair + 2, cols], ALU.max
            )

        def pool_last(pooled, half):
            for ch in range(2):
                cols = slice(ch * CHUNK, (ch + 1) * CHUNK)
                for pair in range(2):
                    nc.vector.tensor_tensor(
                        pooled[:, ch, 2 * pair : 2 * pair + 2, :],
                        late[3, half, pair][:, :, cols],
                        mid[half, pair][:, :, cols],
                        ALU.max,
                    )

        for g in (2, 3):
            for pair in range(2):
                project_late(g, 0, pair, f"bank{2 * (g - 2) + pair}")
        for ch in range(2):
            project_own(ch, f"bank{4 + ch}")
        for pair in range(2):
            pool_mid(0, pair)
        quantize_c(1, c1_bf)
        pooled0 = tile("pooled0", [P, 2, 4, CHUNK], F32)
        pool_last(pooled0, 0)
        summed = {}
        for ch in range(2):
            own_sb = tile(f"own_sb{ch}", [P, 4, CHUNK], F32)
            nc.scalar.copy(own_sb[:], owns[ch][:])
            summed[ch] = tile(f"summed{ch}", [P, 4, CHUNK], F32)
            nc.gpsimd.tensor_tensor(summed[ch][:], own_sb[:], pooled0[:, ch], ALU.add)
        for g in (2, 3):
            for pair in range(2):
                project_late(g, 1, pair, f"bank{2 * (g - 2) + pair}")
        project_own(2, "bank6")
        for pair in range(2):
            pool_mid(1, pair)
        pooled1 = tile("pooled1", [P, 2, 4, CHUNK], F32)
        pool_last(pooled1, 1)
        project_own(3, "bank2")

        def add_own(ch):
            summed[ch] = tile(f"summed{ch}", [P, 4, CHUNK], F32)
            nc.vector.tensor_tensor(summed[ch][:], owns[ch][:], pooled1[:, ch - 2], ALU.add)

        add_own(2)

        wd_bf = tile("wd_bf", [P, N * PACK], BF16)
        for half in range(2):
            nc.scalar.copy(
                wd_bf[:, half * HALF * PACK : (half + 1) * HALF * PACK].rearrange("p (x i t) -> p x t i", i=4, t=PACK),
                wd_raw[:, :, half * HALF : (half + 1) * HALF].rearrange("p t (x i) -> p x t i", i=4),
            )
        wd_codes = tile("wd_codes", [P, N], U32)
        wd_scales = tile("wd_scales", [P, N], U8)
        nc.vector.quantize_mx(wd_codes[:].bitcast(FP8X4), wd_scales[:], wd_bf[:])

        h_bf = {}

        def relu(ch):
            h_bf[ch] = tile(f"h_bf{ch}", [P, CHUNK * PACK], BF16)
            nc.scalar.activation(
                h_bf[ch][:].rearrange("p (x i t) -> p x t i", i=4, t=PACK),
                summed[ch][:].rearrange("p t (x i) -> p x t i", i=4),
                ACT.Relu,
            )

        out_rows = out.rearrange("(u p) j -> p u j", p=P)
        ys = {}

        def second_layer(ch):
            h_codes = tile(f"h_codes{ch}", [P, CHUNK], U32)
            h_scales = tile(f"h_scales{ch}", [P, CHUNK], U8)
            nc.vector.quantize_mx(h_codes[:].bitcast(FP8X4), h_scales[:], h_bf[ch][:])
            ys[ch] = psum.tile([P, 4, CHUNK], F32, name=f"y{ch}", tag=f"bank{(4, 5, 7, 0)[ch]}")
            for u in range(4):
                nc.tensor.matmul_mx(
                    out=ys[ch][:, u, :],
                    lhsT=wd_codes[:, u * P : (u + 1) * P].bitcast(FP8X4),
                    lhsT_scale=wd_scales[:, u * P : (u + 1) * P],
                    rhs=h_codes[:].bitcast(FP8X4),
                    rhs_scale=h_scales[:],
                    start=True,
                    stop=True,
                )

        def finish(ch):
            cols = slice(ch * CHUNK, (ch + 1) * CHUNK)
            res = tile(f"res{ch}", [P, 4, CHUNK], F32)
            step = 2 if ch == 3 else 4
            for u in range(0, 4, step):
                us = slice(u, u + step)
                nc.vector.tensor_tensor(res[:, us, :], ys[ch][:, us, :], gate[:, us, cols], ALU.mult)
                nc.sync.dma_start(out_rows[:, us, cols], res[:, us, :])

        relu(0)
        second_layer(0)
        relu(1)
        second_layer(1)
        add_own(3)
        relu(2)
        second_layer(2)
        finish(0)
        relu(3)
        second_layer(3)
        finish(1)
        finish(2)
        finish(3)
